import numpy as np
import ml_dtypes


def mxq(x, axis, fmt="e4m3"):
    dtype, down = {"e4m3": (ml_dtypes.float8_e4m3fn, 7), "e5m2": (ml_dtypes.float8_e5m2, 14)}[fmt]
    v = np.moveaxis(np.asarray(x, np.float32).astype(ml_dtypes.bfloat16).astype(np.float64), axis, -1)
    blocks = v.reshape(v.shape[:-1] + (-1, 32))
    amax = np.abs(blocks).max(-1, keepdims=True)
    byte = np.maximum(np.where(amax > 0, np.frexp(amax)[1] - 1 + 127, 0) - down, 1)
    scale = np.exp2(byte - 127.0)
    codes = (blocks / scale).astype(np.float32).astype(dtype).astype(np.float64)
    return np.moveaxis((codes * scale).reshape(v.shape), -1, axis)


WIDE = False


def mx_kscale(k):
    if not WIDE:
        return np.ones(k)
    levels = np.array([10, -10, 5, -5, 0])
    if k % 512:
        return np.exp2(np.random.permutation(np.resize(levels, k // 32))).repeat(32)
    a = np.empty((k // 512, 16))
    for p in range(k // 512):
        a[p, :8] = np.random.permutation(np.resize(levels, 8))
        for g in range(8):
            far = levels[np.abs(levels - a[p, g]) >= 10]
            a[p, g + 8] = far[np.random.randint(len(far))]
    return np.exp2(a.ravel()).repeat(32)


def f64(x):
    return np.asarray(x).astype(np.float64)


def striped(idx):
    return np.tile(idx.reshape(-1, 16).T, (8, 1)).astype(np.uint16)


def unstriped(offs):
    return offs[:16].T.reshape(-1).astype(np.int64)


def pack_weight(w):
    k, n = w.shape
    w = f64(np.asarray(w, np.float32).astype(ml_dtypes.bfloat16)).reshape(k // 32, 32, n)
    amax = np.abs(w).max(1)
    byte = np.clip(np.where(amax > 0, np.frexp(amax)[1] - 1 + 127 - 7, 1), 1, 254)
    scaled = (w * np.exp2(127.0 - byte)[:, None, :]).reshape(k, n).astype(np.float32)
    words = np.ascontiguousarray(scaled.reshape(k // 512, 128, 4, n).transpose(0, 1, 3, 2)).astype(ml_dtypes.float8_e4m3fn).view(np.uint8)
    return words, np.ascontiguousarray(byte.astype(np.uint8).reshape(k // 512, 16, n))


def unpack_weight(words, scales):
    g, p, n, _ = words.shape
    vals = np.ascontiguousarray(words).view(ml_dtypes.float8_e4m3fn).astype(np.float64) * np.repeat(np.exp2(scales.astype(np.float64) - 127.0), 8, axis=1)[..., None]
    return vals.transpose(0, 1, 3, 2).reshape(g * 512, n)


E2M1 = np.array([0.0, 0.5, 1.0, 1.5, 2.0, 3.0, 4.0, 6.0, -0.0, -0.5, -1.0, -1.5, -2.0, -3.0, -4.0, -6.0])


def pack_fp4(w):
    k, n = w.shape
    w = f64(np.asarray(w, np.float32).astype(ml_dtypes.bfloat16)).reshape(k // 32, 32, n)
    amax = np.abs(w).max(1)
    mant, ex = np.frexp(amax / 6.0)
    byte = np.clip(np.where(amax > 0, np.where(mant > 0.5, ex, ex - 1) + 127, 1), 1, 254)
    scaled = (w * np.exp2(127.0 - byte)[:, None, :]).reshape(k, n).astype(np.float32)
    c = np.ascontiguousarray(scaled.reshape(k // 512, 128, 4, n).transpose(0, 1, 3, 2)).astype(ml_dtypes.float4_e2m1fn).view(np.uint8) & 0xF
    words = (c[..., 0::2] | (c[..., 1::2] << 4)).reshape(k // 512, 128, 2 * n)
    return np.ascontiguousarray(words), np.ascontiguousarray(byte.astype(np.uint8).reshape(k // 512, 16, n))


def unpack_fp4(words, scales):
    g, _, n = scales.shape
    words = np.ascontiguousarray(words).reshape(g, 128, n, 2)
    nib = np.empty((g, 128, n, 4), np.uint8)
    nib[..., 0::2] = words & 0xF
    nib[..., 1::2] = words >> 4
    vals = E2M1[nib] * np.repeat(np.exp2(scales.astype(np.float64) - 127.0), 8, axis=1)[..., None]
    return vals.transpose(0, 1, 3, 2).reshape(g * 512, n)


def relu(v):
    return np.maximum(v, 0.0)

def planes(y):
    n, m = y.shape
    v = y.astype(np.float32).astype(ml_dtypes.bfloat16).astype(np.float64).reshape(n // 32, 32, m)
    top = np.abs(v).max(1)
    byte = np.clip(np.where(top > 0, np.frexp(top)[1] - 1 + 127 - 7, 1), 1, 254)
    codes = (v * np.exp2(127.0 - byte)[:, None, :]).reshape(n, m).astype(np.float32).astype(ml_dtypes.float8_e4m3fn).view(np.uint8)
    words = codes.reshape(n // 512, 128, 4, m).transpose(0, 1, 3, 2)
    return np.ascontiguousarray(words), np.ascontiguousarray(byte.astype(np.uint8).reshape(n // 512, 16, m))


K, T, S, V, H = 512, 2048, 1024, 512, 512


def setup_inputs():
    n = np.random.standard_normal
    s = mx_kscale(K)[:, None]
    u = mx_kscale(H)
    packed_xT = pack_weight(n((K, T)) * s)
    packed_w2 = pack_fp4(n((H, H)) / np.sqrt(2 * H) / u[:, None])
    packed_w3 = pack_fp4(n((H, H)) / np.sqrt(2 * H) / u[:, None])
    return {
        "x_words": packed_xT[0],
        "x_scales": packed_xT[1],
        "w1": (n((K, H)) / np.sqrt(K) / s * u).astype(np.float32),
        "w2_words": packed_w2[0],
        "w2_scales": packed_w2[1],
        "w3_words": packed_w3[0],
        "w3_scales": packed_w3[1],
        "offs": striped(np.random.permutation(T)[:S]),
    }


def reference(x_words, x_scales, w1, w2_words, w2_scales, w3_words, w3_scales, offs):
    xq = unpack_weight(x_words, x_scales)[:, unstriped(offs)]
    h = relu(mxq(f64(w1), 0, "e4m3").T @ xq)
    low = 0.5 * (h[:, :V] + h[:, V:2 * V])
    high = 0.5 * (h[:, :V] - h[:, V:2 * V])
    out_0 = unpack_fp4(w2_words, w2_scales).T @ mxq(low, 0, "e4m3") + unpack_fp4(w3_words, w3_scales).T @ mxq(high, 0, "e4m3")
    return (out_0,) + planes(out_0)

@@ -1,0 +1,191 @@
+from contextlib import ExitStack
+
+import concourse.mybir as mybir
+
+K, T, S, V, H = 512, 2048, 1024, 512, 512
+FLOPS = 2 * K * H * S + 2 * 2 * H * H * V
+
+F32 = mybir.dt.float32
+BF16 = mybir.dt.bfloat16
+I32 = mybir.dt.int32
+U32 = mybir.dt.uint32
+U16 = mybir.dt.uint16
+U8 = mybir.dt.uint8
+FP8X4 = mybir.dt.float8_e4m3fn_x4
+FP4X4 = mybir.dt.float4_e2m1fn_x4
+ALU = mybir.AluOpType
+ACT = mybir.ActivationFunctionType
+
+P = 128
+PACK = 4
+CHUNK = 128
+CHUNKS = V // CHUNK
+GATHER = 256
+LIST_ROWS = 16
+
+
+def load_scale_rows(queue, plane, rows):
+    for q in range(4):
+        queue.dma_start(out=plane[32 * q : 32 * q + 4, :].bitcast(I32), in_=rows[4 * q : 4 * q + 4, :].bitcast(I32))
+
+
+def tile_picked_haar_relu_po_kernel(
+    tc, x_words, x_scales, w1, w2_words, w2_scales, w3_words, w3_scales, offs, out_0, out_1, out_2
+):
+    nc = tc.nc
+    with ExitStack() as ctx:
+        keep = ctx.enter_context(tc.tile_pool(name="keep", bufs=1))
+        ring = ctx.enter_context(tc.tile_pool(name="ring", bufs=2))
+        psum = ctx.enter_context(tc.psum_pool(name="psum", bufs=2))
+
+        offsets = keep.tile([P, S // LIST_ROWS], U16, name="offsets")
+        x_table = keep.tile([P, T], I32, name="x_table", align_bytes=64)
+        xs_table = keep.tile([P, T], U8, name="xs_table", tag="early_late", align_bytes=64)
+        w1_raw = [keep.tile([P, PACK, H // 2], F32, name="w1_raw%d" % h, align_bytes=64) for h in range(2)]
+        w23s_raw = keep.tile([P, 2, H], U8, name="w23s_raw", align_bytes=64)
+
+        nc.vector.memset(xs_table[:].bitcast(I32), 0)
+        nc.gpsimd.memset(w23s_raw[:].rearrange("p w c -> p (w c)").bitcast(I32), 0)
+
+        nc.sync.dma_start(offsets[:], offs)
+        load_scale_rows(nc.scalar, xs_table, x_scales[0])
+        nc.sync.dma_start(out=x_table[:], in_=x_words[0].rearrange("p c r -> p (c r)").bitcast(I32))
+        w1_rows = w1.rearrange("(p j) c -> p j c", j=PACK)
+        for h in range(2):
+            nc.sync.dma_start(out=w1_raw[h][:], in_=w1_rows[:, :, h * (H // 2) : (h + 1) * (H // 2)])
+        load_scale_rows(nc.sync, w23s_raw[:, 0, :], w2_scales[0])
+        load_scale_rows(nc.gpsimd, w23s_raw[:, 1, :], w3_scales[0])
+
+        xs_picked = keep.tile([P, S], U8, name="xs_picked", align_bytes=64)
+        nc.vector.tensor_copy(xs_picked[:], xs_table[:].indirect(offsets[:]))
+        w23_raw = keep.tile([P, 2, 2 * H], U8, name="w23_raw", tag="early_late", align_bytes=64)
+        for w, words in enumerate((w2_words, w3_words)):
+            nc.sync.dma_start(out=w23_raw[:, w, :].bitcast(I32), in_=words[0].bitcast(I32))
+        x_picked = {}
+        for g in range(V // GATHER):
+            for d in (1, 0):
+                first = d * V + g * GATHER
+                picked = keep.tile([P, GATHER], U32, name="x_picked%d_%d" % (d, g), align_bytes=64)
+                nc.vector.tensor_copy(
+                    picked[:],
+                    x_table[:].bitcast(U32).indirect(offsets[:, first // LIST_ROWS : (first + GATHER) // LIST_ROWS]),
+                )
+                x_picked[d, g] = picked
+
+        w1_bf = keep.tile([P, PACK, P, PACK], BF16, name="w1_bf", tag="w_staged", align_bytes=64)
+        quarter = P // 4
+        for piece in range(4):
+            src = w1_raw[piece // 2][:, :, (piece % 2) * P : (piece % 2 + 1) * P].rearrange("p j (m t) -> p m t j", t=PACK)
+            dst = w1_bf[:, :, piece * quarter : (piece + 1) * quarter, :].rearrange("p t m j -> p m t j")
+            if piece < 3:
+                nc.scalar.activation(out=dst, in_=src, func=ACT.Copy, scale=0.5)
+            else:
+                nc.vector.tensor_scalar(out=dst, in0=src, scalar1=0.5, scalar2=None, op0=ALU.mult)
+        w1_codes = keep.tile([P, H], U32, name="w1_codes", align_bytes=64)
+        w1_scales = keep.tile([P, H], U8, name="w1_scales", align_bytes=64)
+        for t in range(PACK):
+            nc.vector.quantize_mx(
+                out=w1_codes[:, t * P : (t + 1) * P].bitcast(FP8X4),
+                scales=w1_scales[:, t * P : (t + 1) * P],
+                in_=w1_bf[:, t, :, :].rearrange("p m j -> p (m j)"),
+            )
+
+        w23 = keep.tile([P, 2, PACK, 2 * P], U8, name="w23", tag="w_staged", align_bytes=64)
+        w23s = keep.tile([P, 2, PACK, P], U8, name="w23s", tag="early_late", align_bytes=64)
+        nc.vector.tensor_copy(
+            out=w23[:].rearrange("p w t (m b) -> p w t m b", b=2),
+            in_=w23_raw[:].rearrange("p w (m t b) -> p w t m b", t=PACK, b=2),
+        )
+        nc.vector.tensor_copy(out=w23s[:], in_=w23s_raw[:].rearrange("p w (m t) -> p w t m", t=PACK))
+
+        y_codes = keep.tile([P, V], U32, name="y_codes", align_bytes=64)
+        y_scales = keep.tile([P, V], U8, name="y_scales", align_bytes=64)
+        y_rows = out_0.rearrange("(p t) v -> p t v", t=PACK)
+        y_words = out_1[0].rearrange("p c r -> p (c r)").bitcast(I32)
+
+        def first_product(c):
+            banks = {}
+            for d in (1, 0):
+                bank = psum.tile([P, PACK, CHUNK], F32, name="h_bank%d" % d, bufs=3)
+                first = c * CHUNK
+                for t in range(PACK):
+                    nc.tensor.matmul_mx(
+                        out=bank[:, t, :],
+                        lhsT=w1_codes[:, t * P : (t + 1) * P].bitcast(FP8X4),
+                        lhsT_scale=w1_scales[:, t * P : (t + 1) * P],
+                        rhs=x_picked[d, first // GATHER][:, first % GATHER : first % GATHER + CHUNK].bitcast(FP8X4),
+                        rhs_scale=xs_picked[:, d * V + first : d * V + first + CHUNK],
+                        start=True,
+                        stop=True,
+                    )
+                banks[d] = bank
+            half_b = ring.tile([P, CHUNK, PACK], F32, name="half_b", bufs=4)
+            nc.scalar.activation(out=half_b[:], in_=banks[1][:].rearrange("p t v -> p v t"), func=ACT.Relu)
+            return banks[0], half_b
+
+        def bands(bank_a, half_b):
+            band_bf = ring.tile([P, 2, CHUNK, PACK], BF16, name="band_bf", align_bytes=64, bufs=4)
+            for w, op in enumerate((ALU.add, ALU.subtract)):
+                nc.vector.scalar_tensor_tensor(
+                    out=band_bf[:, w, :, :],
+                    in0=bank_a[:].rearrange("p t v -> p v t"),
+                    scalar=0.0,
+                    in1=half_b[:],
+                    op0=ALU.max,
+                    op1=op,
+                )
+            return band_bf
+
+        def second_product(c, band_bf):
+            band_codes = ring.tile([P, 2, CHUNK], U32, name="band_codes", align_bytes=64, bufs=4)
+            band_scales = ring.tile([P, 2, CHUNK], U8, name="band_scales", align_bytes=64, bufs=4)
+            nc.vector.quantize_mx(
+                out=band_codes[:].rearrange("p w v -> p (w v)").bitcast(FP8X4),
+                scales=band_scales[:].rearrange("p w v -> p (w v)"),
+                in_=band_bf[:].rearrange("p w v t -> p (w v t)"),
+            )
+            bank = psum.tile([P, PACK, CHUNK], F32, name="y_bank", bufs=2)
+            for t in range(PACK):
+                for w in range(2):
+                    nc.tensor.matmul_mx(
+                        out=bank[:, t, :],
+                        lhsT=w23[:, w, t, :].bitcast(FP4X4),
+                        lhsT_scale=w23s[:, w, t, :],
+                        rhs=band_codes[:, w, :].bitcast(FP8X4),
+                        rhs_scale=band_scales[:, w, :],
+                        start=(w == 0),
+                        stop=(w == 1),
+                    )
+            cols = slice(c * CHUNK, (c + 1) * CHUNK)
+            y_bf = ring.tile([P, CHUNK, PACK], BF16, name="y_bf", align_bytes=64, bufs=4)
+            nc.scalar.copy(out=y_bf[:], in_=bank[:].rearrange("p t v -> p v t"))
+            y_f32 = ring.tile([P, PACK, CHUNK], F32, name="y_f32", bufs=4)
+            nc.scalar.copy(out=y_f32[:], in_=bank[:])
+            nc.sync.dma_start(out=y_rows[:, :, cols], in_=y_f32[:])
+            return y_bf
+
+        def planes(c, y_bf):
+            cols = slice(c * CHUNK, (c + 1) * CHUNK)
+            nc.vector.quantize_mx(
+                out=y_codes[:, cols].bitcast(FP8X4),
+                scales=y_scales[:, cols],
+                in_=y_bf[:].rearrange("p v t -> p (v t)"),
+            )
+            nc.sync.dma_start(out=y_words[:, cols], in_=y_codes[:, cols].bitcast(I32))
+
+        hidden = [first_product(c) for c in range(2)]
+        band = [bands(*hidden[0])]
+        y_bf_all = []
+        for c in range(CHUNKS):
+            if c + 2 < CHUNKS:
+                hidden.append(first_product(c + 2))
+            if c + 1 < CHUNKS:
+                band.append(bands(*hidden[c + 1]))
+            y_bf_all.append(second_product(c, band[c]))
+        for c in range(CHUNKS):
+            planes(c, y_bf_all[c])
+        for q in range(4):
+            queue = nc.sync if q % 2 == 0 else nc.scalar
+            queue.dma_start(
+                out=out_2[0, 4 * q : 4 * q + 4, :].bitcast(I32), in_=y_scales[32 * q : 32 * q + 4, :].bitcast(I32)
+            )

@@ -24,8 +24,8 @@ GATHER = 256
 LIST_ROWS = 16
 
 
-def load_scale_rows(queue, plane, rows):
-    for q in range(4):
+def load_scale_rows(queue, plane, rows, quadrants):
+    for q in quadrants:
         queue.dma_start(out=plane[32 * q : 32 * q + 4, :].bitcast(I32), in_=rows[4 * q : 4 * q + 4, :].bitcast(I32))
 
 
@@ -40,27 +40,50 @@ def tile_picked_haar_relu_po_kernel(
 
         offsets = keep.tile([P, S // LIST_ROWS], U16, name="offsets")
         x_table = keep.tile([P, T], I32, name="x_table", align_bytes=64)
-        xs_table = keep.tile([P, T], U8, name="xs_table", tag="early_late", align_bytes=64)
+        xs_table = keep.tile([P, T], U8, name="xs_table", align_bytes=64)
         w1_raw = [keep.tile([P, PACK, H // 2], F32, name="w1_raw%d" % h, align_bytes=64) for h in range(2)]
+        w23_raw = keep.tile([P, 2, 2 * H], U8, name="w23_raw", align_bytes=64)
         w23s_raw = keep.tile([P, 2, H], U8, name="w23s_raw", align_bytes=64)
 
         nc.vector.memset(xs_table[:].bitcast(I32), 0)
-        nc.gpsimd.memset(w23s_raw[:].rearrange("p w c -> p (w c)").bitcast(I32), 0)
 
+        nc.gpsimd.memset(w23s_raw[:].rearrange("p w c -> p (w c)").bitcast(I32), 0)
         nc.sync.dma_start(offsets[:], offs)
-        load_scale_rows(nc.scalar, xs_table, x_scales[0])
-        nc.sync.dma_start(out=x_table[:], in_=x_words[0].rearrange("p c r -> p (c r)").bitcast(I32))
+        for w, words in enumerate((w2_words, w3_words)):
+            nc.sync.dma_start(out=w23_raw[:, w, :].bitcast(I32), in_=words[0].bitcast(I32))
         w1_rows = w1.rearrange("(p j) c -> p j c", j=PACK)
         for h in range(2):
             nc.sync.dma_start(out=w1_raw[h][:], in_=w1_rows[:, :, h * (H // 2) : (h + 1) * (H // 2)])
-        load_scale_rows(nc.sync, w23s_raw[:, 0, :], w2_scales[0])
-        load_scale_rows(nc.gpsimd, w23s_raw[:, 1, :], w3_scales[0])
+            if h == 0:
+                load_scale_rows(nc.sync, xs_table, x_scales[0], range(4))
+        load_scale_rows(nc.sync, w23s_raw[:, 0, :], w2_scales[0], range(0, 1))
+        nc.sync.dma_start(out=x_table[:], in_=x_words[0].rearrange("p c r -> p (c r)").bitcast(I32))
+        load_scale_rows(nc.sync, w23s_raw[:, 0, :], w2_scales[0], range(1, 4))
+        load_scale_rows(nc.sync, w23s_raw[:, 1, :], w3_scales[0], range(4))
+
+        w23 = keep.tile([P, 2, PACK, 2 * P], U8, name="w23", align_bytes=64)
+        nc.vector.tensor_copy(
+            out=w23[:].rearrange("p w t (m b) -> p w t m b", b=2),
+            in_=w23_raw[:].rearrange("p w (m t b) -> p w t m b", t=PACK, b=2),
+        )
 
         xs_picked = keep.tile([P, S], U8, name="xs_picked", align_bytes=64)
         nc.vector.tensor_copy(xs_picked[:], xs_table[:].indirect(offsets[:]))
-        w23_raw = keep.tile([P, 2, 2 * H], U8, name="w23_raw", tag="early_late", align_bytes=64)
-        for w, words in enumerate((w2_words, w3_words)):
-            nc.sync.dma_start(out=w23_raw[:, w, :].bitcast(I32), in_=words[0].bitcast(I32))
+
+        w1_bf = keep.tile([P, PACK, P, PACK], BF16, name="w1_bf", align_bytes=64)
+        for h in range(2):
+            nc.scalar.activation(
+                out=w1_bf[:, :, h * (P // 2) : (h + 1) * (P // 2), :].rearrange("p t m j -> p m t j"),
+                in_=w1_raw[h][:].rearrange("p j (m t) -> p m t j", t=PACK),
+                func=ACT.Copy,
+                scale=0.5,
+            )
+        w1_codes = keep.tile([P, H], U32, name="w1_codes", align_bytes=64)
+        w1_scales = keep.tile([P, H], U8, name="w1_scales", align_bytes=64)
+        nc.vector.quantize_mx(
+            out=w1_codes[:].bitcast(FP8X4), scales=w1_scales[:], in_=w1_bf[:].rearrange("p t m j -> p (t m j)")
+        )
+
         x_picked = {}
         for g in range(V // GATHER):
             for d in (1, 0):
@@ -72,30 +95,7 @@ def tile_picked_haar_relu_po_kernel(
                 )
                 x_picked[d, g] = picked
 
-        w1_bf = keep.tile([P, PACK, P, PACK], BF16, name="w1_bf", tag="w_staged", align_bytes=64)
-        quarter = P // 4
-        for piece in range(4):
-            src = w1_raw[piece // 2][:, :, (piece % 2) * P : (piece % 2 + 1) * P].rearrange("p j (m t) -> p m t j", t=PACK)
-            dst = w1_bf[:, :, piece * quarter : (piece + 1) * quarter, :].rearrange("p t m j -> p m t j")
-            if piece < 3:
-                nc.scalar.activation(out=dst, in_=src, func=ACT.Copy, scale=0.5)
-            else:
-                nc.vector.tensor_scalar(out=dst, in0=src, scalar1=0.5, scalar2=None, op0=ALU.mult)
-        w1_codes = keep.tile([P, H], U32, name="w1_codes", align_bytes=64)
-        w1_scales = keep.tile([P, H], U8, name="w1_scales", align_bytes=64)
-        for t in range(PACK):
-            nc.vector.quantize_mx(
-                out=w1_codes[:, t * P : (t + 1) * P].bitcast(FP8X4),
-                scales=w1_scales[:, t * P : (t + 1) * P],
-                in_=w1_bf[:, t, :, :].rearrange("p m j -> p (m j)"),
-            )
-
-        w23 = keep.tile([P, 2, PACK, 2 * P], U8, name="w23", tag="w_staged", align_bytes=64)
-        w23s = keep.tile([P, 2, PACK, P], U8, name="w23s", tag="early_late", align_bytes=64)
-        nc.vector.tensor_copy(
-            out=w23[:].rearrange("p w t (m b) -> p w t m b", b=2),
-            in_=w23_raw[:].rearrange("p w (m t b) -> p w t m b", t=PACK, b=2),
-        )
+        w23s = keep.tile([P, 2, PACK, P], U8, name="w23s", align_bytes=64)
         nc.vector.tensor_copy(out=w23s[:], in_=w23s_raw[:].rearrange("p w (m t) -> p w t m", t=PACK))
 
         y_codes = keep.tile([P, V], U32, name="y_codes", align_bytes=64)
@@ -123,18 +123,16 @@ def tile_picked_haar_relu_po_kernel(
             nc.scalar.activation(out=half_b[:], in_=banks[1][:].rearrange("p t v -> p v t"), func=ACT.Relu)
             return banks[0], half_b
 
-        def bands(bank_a, half_b):
-            band_bf = ring.tile([P, 2, CHUNK, PACK], BF16, name="band_bf", align_bytes=64, bufs=4)
-            for w, op in enumerate((ALU.add, ALU.subtract)):
-                nc.vector.scalar_tensor_tensor(
-                    out=band_bf[:, w, :, :],
-                    in0=bank_a[:].rearrange("p t v -> p v t"),
-                    scalar=0.0,
-                    in1=half_b[:],
-                    op0=ALU.max,
-                    op1=op,
-                )
-            return band_bf
+        def band(w, hidden, band_bf):
+            bank_a, half_b = hidden
+            nc.vector.scalar_tensor_tensor(
+                out=band_bf[:, w, :, :],
+                in0=bank_a[:].rearrange("p t v -> p v t"),
+                scalar=0.0,
+                in1=half_b[:],
+                op0=ALU.max,
+                op1=(ALU.add, ALU.subtract)[w],
+            )
 
         def second_product(c, band_bf):
             band_codes = ring.tile([P, 2, CHUNK], U32, name="band_codes", align_bytes=64, bufs=4)
@@ -157,35 +155,41 @@ def tile_picked_haar_relu_po_kernel(
                         stop=(w == 1),
                     )
             cols = slice(c * CHUNK, (c + 1) * CHUNK)
-            y_bf = ring.tile([P, CHUNK, PACK], BF16, name="y_bf", align_bytes=64, bufs=4)
-            nc.scalar.copy(out=y_bf[:], in_=bank[:].rearrange("p t v -> p v t"))
             y_f32 = ring.tile([P, PACK, CHUNK], F32, name="y_f32", bufs=4)
-            nc.scalar.copy(out=y_f32[:], in_=bank[:])
-            nc.sync.dma_start(out=y_rows[:, :, cols], in_=y_f32[:])
-            return y_bf
+            if c + 1 < CHUNKS:
+                nc.scalar.copy(out=y_f32[:], in_=bank[:])
+                nc.sync.dma_start(out=y_rows[:, :, cols], in_=y_f32[:])
+                nc.scalar.copy(out=y_bf[:, cols, :], in_=bank[:].rearrange("p t v -> p v t"))
+            else:
+                nc.vector.tensor_copy(out=y_bf[:, cols, :], in_=bank[:].rearrange("p t v -> p v t"))
+                nc.scalar.copy(out=y_f32[:], in_=bank[:])
+                nc.scalar.dma_start(out=y_rows[:, :, cols], in_=y_f32[:])
 
-        def planes(c, y_bf):
-            cols = slice(c * CHUNK, (c + 1) * CHUNK)
+        def planes(cols):
             nc.vector.quantize_mx(
                 out=y_codes[:, cols].bitcast(FP8X4),
                 scales=y_scales[:, cols],
-                in_=y_bf[:].rearrange("p v t -> p (v t)"),
+                in_=y_bf[:, cols, :].rearrange("p v t -> p (v t)"),
             )
             nc.sync.dma_start(out=y_words[:, cols], in_=y_codes[:, cols].bitcast(I32))
 
-        hidden = [first_product(c) for c in range(2)]
-        band = [bands(*hidden[0])]
-        y_bf_all = []
+        y_bf = keep.tile([P, V, PACK], BF16, name="y_bf", align_bytes=64)
+        hidden = [first_product(c) for c in range(3)]
+        band_bf = [
+            ring.tile([P, 2, CHUNK, PACK], BF16, name="band_bf", align_bytes=64, bufs=4) for c in range(CHUNKS)
+        ]
         for c in range(CHUNKS):
-            if c + 2 < CHUNKS:
-                hidden.append(first_product(c + 2))
-            if c + 1 < CHUNKS:
-                band.append(bands(*hidden[c + 1]))
-            y_bf_all.append(second_product(c, band[c]))
-        for c in range(CHUNKS):
-            planes(c, y_bf_all[c])
+            band(0, hidden[c], band_bf[c])
+            if c > 0:
+                second_product(c - 1, band_bf[c - 1])
+            band(1, hidden[c], band_bf[c])
+            if c + 3 < CHUNKS:
+                hidden.append(first_product(c + 3))
+        second_product(CHUNKS - 1, band_bf[CHUNKS - 1])
+        for first, last in ((0, 2), (2, 3), (3, 4)):
+            planes(slice(first * CHUNK, last * CHUNK))
         for q in range(4):
-            queue = nc.sync if q % 2 == 0 else nc.scalar
+            queue = nc.sync if q < 2 else nc.scalar
             queue.dma_start(
                 out=out_2[0, 4 * q : 4 * q + 4, :].bitcast(I32), in_=y_scales[32 * q : 32 * q + 4, :].bitcast(I32)
             )

@@ -39,7 +39,7 @@ def tile_picked_haar_relu_po_kernel(
         psum = ctx.enter_context(tc.psum_pool(name="psum", bufs=2))
 
         offsets = keep.tile([P, S // LIST_ROWS], U16, name="offsets")
-        x_table = keep.tile([P, T], I32, name="x_table", align_bytes=64)
+        x_table = keep.tile([P, T], I32, name="x_table", tag="x_table", align_bytes=64)
         xs_table = keep.tile([P, T], U8, name="xs_table", align_bytes=64)
         w1_raw = [keep.tile([P, PACK, H // 2], F32, name="w1_raw%d" % h, align_bytes=64) for h in range(2)]
         w23_raw = keep.tile([P, 2, 2 * H], U8, name="w23_raw", align_bytes=64)
@@ -95,8 +95,8 @@ def tile_picked_haar_relu_po_kernel(
                 )
                 x_picked[d, g] = picked
 
-        w23s = keep.tile([P, 2, PACK, P], U8, name="w23s", align_bytes=64)
-        nc.vector.tensor_copy(out=w23s[:], in_=w23s_raw[:].rearrange("p w (m t) -> p w t m", t=PACK))
+        w23s = keep.tile([P, 2, PACK, P], U8, name="w23s", tag="x_table", align_bytes=64)
+        nc.gpsimd.tensor_copy(out=w23s[:], in_=w23s_raw[:].rearrange("p w (m t) -> p w t m", t=PACK))
 
         y_codes = keep.tile([P, V], U32, name="y_codes", align_bytes=64)
         y_scales = keep.tile([P, V], U8, name="y_scales", align_bytes=64)
@@ -156,14 +156,48 @@ def tile_picked_haar_relu_po_kernel(
                     )
             cols = slice(c * CHUNK, (c + 1) * CHUNK)
             y_f32 = ring.tile([P, PACK, CHUNK], F32, name="y_f32", bufs=4)
-            if c + 1 < CHUNKS:
-                nc.scalar.copy(out=y_f32[:], in_=bank[:])
-                nc.sync.dma_start(out=y_rows[:, :, cols], in_=y_f32[:])
-                nc.scalar.copy(out=y_bf[:, cols, :], in_=bank[:].rearrange("p t v -> p v t"))
-            else:
-                nc.vector.tensor_copy(out=y_bf[:, cols, :], in_=bank[:].rearrange("p t v -> p v t"))
-                nc.scalar.copy(out=y_f32[:], in_=bank[:])
-                nc.scalar.dma_start(out=y_rows[:, :, cols], in_=y_f32[:])
+            nc.scalar.copy(out=y_f32[:], in_=bank[:])
+            nc.sync.dma_start(out=y_rows[:, :, cols], in_=y_f32[:])
+            return bank
+
+        def round_from_bank(c, bank):
+            nc.scalar.copy(out=y_bf[:, c * CHUNK : (c + 1) * CHUNK, :], in_=bank[:].rearrange("p t v -> p v t"))
+
+        def last_second_product(band_bf):
+            cols = slice(V - CHUNK, V)
+            banks = [
+                psum.tile([P, PACK, CHUNK], F32, name="h_bank%d" % d, bufs=3)[:, 0, :] for d in (1, 0, 1, 0)
+            ]
+            for w in range(2):
+                codes = keep.tile([P, CHUNK], U32, name="last_codes%d" % w, align_bytes=64)
+                scales = keep.tile([P, CHUNK], U8, name="last_scales%d" % w, align_bytes=64)
+                nc.vector.quantize_mx(
+                    out=codes[:].bitcast(FP8X4), scales=scales[:], in_=band_bf[:, w, :, :].rearrange("p v t -> p (v t)")
+                )
+                for t in range(PACK):
+                    nc.tensor.matmul_mx(
+                        out=banks[t],
+                        lhsT=w23[:, w, t, :].bitcast(FP4X4),
+                        lhsT_scale=w23s[:, w, t, :],
+                        rhs=codes[:].bitcast(FP8X4),
+                        rhs_scale=scales[:],
+                        start=(w == 0),
+                        stop=(w == 1),
+                    )
+                if w == 0:
+                    band(1, hidden[CHUNKS - 1], band_bf)
+            y_f32 = ring.tile([P, PACK, CHUNK], F32, name="y_f32", bufs=4)
+            for t in range(PACK):
+                if t < 2:
+                    nc.scalar.copy(out=y_f32[:, t, :], in_=banks[t])
+                else:
+                    nc.vector.tensor_copy(out=y_f32[:, t, :], in_=banks[t])
+            nc.scalar.dma_start(out=y_rows[:, 0:2, cols], in_=y_f32[:, 0:2, :])
+            nc.sync.dma_start(out=y_rows[:, 2:4, cols], in_=y_f32[:, 2:4, :])
+            nc.vector.tensor_copy(
+                out=y_bf[:, cols, :].rearrange("p (u i) t -> p u t i", i=PACK),
+                in_=y_f32[:].rearrange("p t (u i) -> p u t i", i=PACK),
+            )
 
         def planes(cols):
             nc.vector.quantize_mx(
@@ -181,12 +215,16 @@ def tile_picked_haar_relu_po_kernel(
         for c in range(CHUNKS):
             band(0, hidden[c], band_bf[c])
             if c > 0:
-                second_product(c - 1, band_bf[c - 1])
-            band(1, hidden[c], band_bf[c])
+                y_bank = second_product(c - 1, band_bf[c - 1])
+                if c + 1 < CHUNKS:
+                    round_from_bank(c - 1, y_bank)
+            if c + 1 < CHUNKS:
+                band(1, hidden[c], band_bf[c])
             if c + 3 < CHUNKS:
                 hidden.append(first_product(c + 3))
-        second_product(CHUNKS - 1, band_bf[CHUNKS - 1])
-        for first, last in ((0, 2), (2, 3), (3, 4)):
+        last_second_product(band_bf[CHUNKS - 1])
+        round_from_bank(CHUNKS - 2, y_bank)
+        for first, last in ((0, 2), (2, 4)):
             planes(slice(first * CHUNK, last * CHUNK))
         for q in range(4):
             queue = nc.sync if q < 2 else nc.scalar

@@ -62,10 +62,11 @@ def tile_picked_haar_relu_po_kernel(
         load_scale_rows(nc.sync, w23s_raw[:, 1, :], w3_scales[0], range(4))
 
         w23 = keep.tile([P, 2, PACK, 2 * P], U8, name="w23", align_bytes=64)
-        nc.vector.tensor_copy(
-            out=w23[:].rearrange("p w t (m b) -> p w t m b", b=2),
-            in_=w23_raw[:].rearrange("p w (m t b) -> p w t m b", t=PACK, b=2),
-        )
+        for w in range(2):
+            nc.gpsimd.tensor_copy(
+                out=w23[:, w].rearrange("p t (m b) -> p t m b", b=2),
+                in_=w23_raw[:, w].rearrange("p (m t b) -> p t m b", t=PACK, b=2),
+            )
 
         xs_picked = keep.tile([P, S], U8, name="xs_picked", align_bytes=64)
         nc.vector.tensor_copy(xs_picked[:], xs_table[:].indirect(offsets[:]))

@@ -22,11 +22,14 @@ CHUNK = 128
 CHUNKS = V // CHUNK
 GATHER = 256
 LIST_ROWS = 16
+SPREAD = 8
 
 
-def load_scale_rows(queue, plane, rows, quadrants):
-    for q in quadrants:
-        queue.dma_start(out=plane[32 * q : 32 * q + 4, :].bitcast(I32), in_=rows[4 * q : 4 * q + 4, :].bitcast(I32))
+def place_scale_rows(queue, plane, spread):
+    for q in range(4):
+        queue.dma_start(
+            out=plane[32 * q : 32 * q + 4, :].bitcast(I32), in_=spread[32 * q : 32 * q + 32 : SPREAD, :].bitcast(I32)
+        )
 
 
 def tile_picked_haar_relu_po_kernel(
@@ -40,36 +43,39 @@ def tile_picked_haar_relu_po_kernel(
 
         offsets = keep.tile([P, S // LIST_ROWS], U16, name="offsets")
         x_table = keep.tile([P, T], I32, name="x_table", tag="x_table", align_bytes=64)
-        xs_table = keep.tile([P, T], U8, name="xs_table", align_bytes=64)
+        xs_table = keep.tile([P, T], U8, name="xs_table", tag="xs_table", align_bytes=64)
         w1_raw = [keep.tile([P, PACK, H // 2], F32, name="w1_raw%d" % h, align_bytes=64) for h in range(2)]
-        w23_raw = keep.tile([P, 2, 2 * H], U8, name="w23_raw", align_bytes=64)
         w23s_raw = keep.tile([P, 2, H], U8, name="w23s_raw", align_bytes=64)
+        xs_plane = keep.tile([P, S], U8, name="xs_plane", align_bytes=64)
+        w23s = keep.tile([P, 2, PACK, P], U8, name="w23s", align_bytes=64)
 
         nc.vector.memset(xs_table[:].bitcast(I32), 0)
-
         nc.gpsimd.memset(w23s_raw[:].rearrange("p w c -> p (w c)").bitcast(I32), 0)
+        nc.gpsimd.memset(xs_plane[:].bitcast(I32), 0)
+        nc.gpsimd.memset(w23s[:].rearrange("p w t m -> p (w t m)").bitcast(I32), 0)
+
         nc.sync.dma_start(offsets[:], offs)
-        for w, words in enumerate((w2_words, w3_words)):
-            nc.sync.dma_start(out=w23_raw[:, w, :].bitcast(I32), in_=words[0].bitcast(I32))
         w1_rows = w1.rearrange("(p j) c -> p j c", j=PACK)
         for h in range(2):
             nc.sync.dma_start(out=w1_raw[h][:], in_=w1_rows[:, :, h * (H // 2) : (h + 1) * (H // 2)])
-            if h == 0:
-                load_scale_rows(nc.sync, xs_table, x_scales[0], range(4))
-        load_scale_rows(nc.sync, w23s_raw[:, 0, :], w2_scales[0], range(0, 1))
         nc.sync.dma_start(out=x_table[:], in_=x_words[0].rearrange("p c r -> p (c r)").bitcast(I32))
-        load_scale_rows(nc.sync, w23s_raw[:, 0, :], w2_scales[0], range(1, 4))
-        load_scale_rows(nc.sync, w23s_raw[:, 1, :], w3_scales[0], range(4))
+        nc.scalar.dma_start(out=xs_table[0:P:SPREAD, :].bitcast(I32), in_=x_scales[0].bitcast(I32))
+        for w, scales in enumerate((w2_scales, w3_scales)):
+            nc.scalar.dma_start(out=w23s_raw[0:P:SPREAD, w, :].bitcast(I32), in_=scales[0].bitcast(I32))
 
-        w23 = keep.tile([P, 2, PACK, 2 * P], U8, name="w23", align_bytes=64)
-        for w in range(2):
-            nc.gpsimd.tensor_copy(
-                out=w23[:, w].rearrange("p t (m b) -> p t m b", b=2),
-                in_=w23_raw[:, w].rearrange("p (m t b) -> p t m b", t=PACK, b=2),
-            )
+        w23s_dealt = keep.tile([P, 2, PACK, P], U8, name="w23s_dealt", align_bytes=64)
+        nc.vector.tensor_copy(out=w23s_dealt[:], in_=w23s_raw[:].rearrange("p w (m t) -> p w t m", t=PACK))
 
         xs_picked = keep.tile([P, S], U8, name="xs_picked", align_bytes=64)
         nc.vector.tensor_copy(xs_picked[:], xs_table[:].indirect(offsets[:]))
+        place_scale_rows(nc.sync, xs_plane[:], xs_picked[:])
+
+        w23_raw = keep.tile([P, 2, 2 * H], U8, name="w23_raw", tag="xs_table", align_bytes=64)
+        for w, words in enumerate((w2_words, w3_words)):
+            nc.sync.dma_start(out=w23_raw[:, w, :].bitcast(I32), in_=words[0].bitcast(I32))
+        place_scale_rows(
+            nc.sync, w23s[:].rearrange("p w t m -> p (w t m)"), w23s_dealt[:].rearrange("p w t m -> p (w t m)")
+        )
 
         w1_bf = keep.tile([P, PACK, P, PACK], BF16, name="w1_bf", align_bytes=64)
         for h in range(2):
@@ -96,8 +102,12 @@ def tile_picked_haar_relu_po_kernel(
                 )
                 x_picked[d, g] = picked
 
-        w23s = keep.tile([P, 2, PACK, P], U8, name="w23s", tag="x_table", align_bytes=64)
-        nc.gpsimd.tensor_copy(out=w23s[:], in_=w23s_raw[:].rearrange("p w (m t) -> p w t m", t=PACK))
+        w23 = keep.tile([P, 2, PACK, 2 * P], U8, name="w23", tag="x_table", align_bytes=64)
+        for w in range(2):
+            nc.gpsimd.tensor_copy(
+                out=w23[:, w].rearrange("p t c -> p (t c)").bitcast(U16).rearrange("p (t m) -> p t m", t=PACK),
+                in_=w23_raw[:, w].bitcast(U16).rearrange("p (m t) -> p t m", t=PACK),
+            )
 
         y_codes = keep.tile([P, V], U32, name="y_codes", align_bytes=64)
         y_scales = keep.tile([P, V], U8, name="y_scales", align_bytes=64)
@@ -115,7 +125,7 @@ def tile_picked_haar_relu_po_kernel(
                         lhsT=w1_codes[:, t * P : (t + 1) * P].bitcast(FP8X4),
                         lhsT_scale=w1_scales[:, t * P : (t + 1) * P],
                         rhs=x_picked[d, first // GATHER][:, first % GATHER : first % GATHER + CHUNK].bitcast(FP8X4),
-                        rhs_scale=xs_picked[:, d * V + first : d * V + first + CHUNK],
+                        rhs_scale=xs_plane[:, d * V + first : d * V + first + CHUNK],
                         start=True,
                         stop=True,
                     )

@@ -63,12 +63,12 @@ def tile_picked_haar_relu_po_kernel(
         for w, scales in enumerate((w2_scales, w3_scales)):
             nc.scalar.dma_start(out=w23s_raw[0:P:SPREAD, w, :].bitcast(I32), in_=scales[0].bitcast(I32))
 
-        w23s_dealt = keep.tile([P, 2, PACK, P], U8, name="w23s_dealt", align_bytes=64)
-        nc.vector.tensor_copy(out=w23s_dealt[:], in_=w23s_raw[:].rearrange("p w (m t) -> p w t m", t=PACK))
-
         xs_picked = keep.tile([P, S], U8, name="xs_picked", align_bytes=64)
         nc.vector.tensor_copy(xs_picked[:], xs_table[:].indirect(offsets[:]))
         place_scale_rows(nc.sync, xs_plane[:], xs_picked[:])
+
+        w23s_dealt = keep.tile([P, 2, PACK, P], U8, name="w23s_dealt", align_bytes=64)
+        nc.vector.tensor_copy(out=w23s_dealt[:], in_=w23s_raw[:].rearrange("p w (m t) -> p w t m", t=PACK))
 
         w23_raw = keep.tile([P, 2, 2 * H], U8, name="w23_raw", tag="xs_table", align_bytes=64)
         for w, words in enumerate((w2_words, w3_words)):
@@ -77,7 +77,7 @@ def tile_picked_haar_relu_po_kernel(
             nc.sync, w23s[:].rearrange("p w t m -> p (w t m)"), w23s_dealt[:].rearrange("p w t m -> p (w t m)")
         )
 
-        w1_bf = keep.tile([P, PACK, P, PACK], BF16, name="w1_bf", align_bytes=64)
+        w1_bf = keep.tile([P, PACK, P, PACK], BF16, name="w1_bf", tag="w1_bf", align_bytes=64)
         for h in range(2):
             nc.scalar.activation(
                 out=w1_bf[:, :, h * (P // 2) : (h + 1) * (P // 2), :].rearrange("p t m j -> p m t j"),
@@ -91,16 +91,14 @@ def tile_picked_haar_relu_po_kernel(
             out=w1_codes[:].bitcast(FP8X4), scales=w1_scales[:], in_=w1_bf[:].rearrange("p t m j -> p (t m j)")
         )
 
-        x_picked = {}
+        x_picked = keep.tile([P, S], U32, name="x_picked", tag="w1_bf", align_bytes=64)
         for g in range(V // GATHER):
             for d in (1, 0):
                 first = d * V + g * GATHER
-                picked = keep.tile([P, GATHER], U32, name="x_picked%d_%d" % (d, g), align_bytes=64)
                 nc.vector.tensor_copy(
-                    picked[:],
+                    x_picked[:, first : first + GATHER],
                     x_table[:].bitcast(U32).indirect(offsets[:, first // LIST_ROWS : (first + GATHER) // LIST_ROWS]),
                 )
-                x_picked[d, g] = picked
 
         w23 = keep.tile([P, 2, PACK, 2 * P], U8, name="w23", tag="x_table", align_bytes=64)
         for w in range(2):
@@ -124,7 +122,7 @@ def tile_picked_haar_relu_po_kernel(
                         out=bank[:, t, :],
                         lhsT=w1_codes[:, t * P : (t + 1) * P].bitcast(FP8X4),
                         lhsT_scale=w1_scales[:, t * P : (t + 1) * P],
-                        rhs=x_picked[d, first // GATHER][:, first % GATHER : first % GATHER + CHUNK].bitcast(FP8X4),
+                        rhs=x_picked[:, d * V + first : d * V + first + CHUNK].bitcast(FP8X4),
                         rhs_scale=xs_plane[:, d * V + first : d * V + first + CHUNK],
                         start=True,
                         stop=True,
@@ -169,12 +167,18 @@ def tile_picked_haar_relu_po_kernel(
             y_f32 = ring.tile([P, PACK, CHUNK], F32, name="y_f32", bufs=4)
             nc.scalar.copy(out=y_f32[:], in_=bank[:])
             nc.sync.dma_start(out=y_rows[:, :, cols], in_=y_f32[:])
-            return bank
+            return bank, y_f32
 
         def round_from_bank(c, bank):
             nc.scalar.copy(out=y_bf[:, c * CHUNK : (c + 1) * CHUNK, :], in_=bank[:].rearrange("p t v -> p v t"))
 
-        def last_second_product(band_bf):
+        def round_from_sbuf(c, y_f32):
+            nc.vector.tensor_copy(
+                out=y_bf[:, c * CHUNK : (c + 1) * CHUNK, :].rearrange("p (u i) t -> p u t i", i=PACK),
+                in_=y_f32[:].rearrange("p t (u i) -> p u t i", i=PACK),
+            )
+
+        def last_second_product(band_bf, y_before):
             cols = slice(V - CHUNK, V)
             banks = [
                 psum.tile([P, PACK, CHUNK], F32, name="h_bank%d" % d, bufs=3)[:, 0, :] for d in (1, 0, 1, 0)
@@ -197,18 +201,21 @@ def tile_picked_haar_relu_po_kernel(
                     )
                 if w == 0:
                     band(1, hidden[CHUNKS - 1], band_bf)
+                    planes(slice(0, CHUNK))
+            planes(slice(CHUNK, 2 * CHUNK))
+            round_from_sbuf(CHUNKS - 2, y_before)
+            planes(slice(2 * CHUNK, 3 * CHUNK))
+            store_codes(slice(0, 3 * CHUNK))
             y_f32 = ring.tile([P, PACK, CHUNK], F32, name="y_f32", bufs=4)
             for t in range(PACK):
                 if t < 2:
                     nc.scalar.copy(out=y_f32[:, t, :], in_=banks[t])
                 else:
                     nc.vector.tensor_copy(out=y_f32[:, t, :], in_=banks[t])
-            nc.scalar.dma_start(out=y_rows[:, 0:2, cols], in_=y_f32[:, 0:2, :])
-            nc.sync.dma_start(out=y_rows[:, 2:4, cols], in_=y_f32[:, 2:4, :])
-            nc.vector.tensor_copy(
-                out=y_bf[:, cols, :].rearrange("p (u i) t -> p u t i", i=PACK),
-                in_=y_f32[:].rearrange("p t (u i) -> p u t i", i=PACK),
-            )
+            nc.scalar.dma_start(out=y_rows[:, :, cols], in_=y_f32[:])
+            round_from_sbuf(CHUNKS - 1, y_f32)
+            planes(cols)
+            store_codes(cols)
 
         def planes(cols):
             nc.vector.quantize_mx(
@@ -216,6 +223,8 @@ def tile_picked_haar_relu_po_kernel(
                 scales=y_scales[:, cols],
                 in_=y_bf[:, cols, :].rearrange("p v t -> p (v t)"),
             )
+
+        def store_codes(cols):
             nc.sync.dma_start(out=y_words[:, cols], in_=y_codes[:, cols].bitcast(I32))
 
         y_bf = keep.tile([P, V, PACK], BF16, name="y_bf", align_bytes=64)
@@ -226,17 +235,14 @@ def tile_picked_haar_relu_po_kernel(
         for c in range(CHUNKS):
             band(0, hidden[c], band_bf[c])
             if c > 0:
-                y_bank = second_product(c - 1, band_bf[c - 1])
+                y_bank, y_f32 = second_product(c - 1, band_bf[c - 1])
                 if c + 1 < CHUNKS:
                     round_from_bank(c - 1, y_bank)
             if c + 1 < CHUNKS:
                 band(1, hidden[c], band_bf[c])
             if c + 3 < CHUNKS:
                 hidden.append(first_product(c + 3))
-        last_second_product(band_bf[CHUNKS - 1])
-        round_from_bank(CHUNKS - 2, y_bank)
-        for first, last in ((0, 2), (2, 4)):
-            planes(slice(first * CHUNK, last * CHUNK))
+        last_second_product(band_bf[CHUNKS - 1], y_f32)
         for q in range(4):
             queue = nc.sync if q < 2 else nc.scalar
             queue.dma_start(

@@ -23,6 +23,7 @@ CHUNKS = V // CHUNK
 GATHER = 256
 LIST_ROWS = 16
 SPREAD = 8
+W1_FIRST = 256
 
 
 def place_scale_rows(queue, plane, spread):
@@ -44,44 +45,59 @@ def tile_picked_haar_relu_po_kernel(
         offsets = keep.tile([P, S // LIST_ROWS], U16, name="offsets")
         x_table = keep.tile([P, T], I32, name="x_table", tag="x_table", align_bytes=64)
         xs_table = keep.tile([P, T], U8, name="xs_table", tag="xs_table", align_bytes=64)
-        w1_raw = [keep.tile([P, PACK, H // 2], F32, name="w1_raw%d" % h, align_bytes=64) for h in range(2)]
+        w1_raw = [
+            keep.tile([P, PACK, width], F32, name="w1_raw%d" % h, align_bytes=64)
+            for h, width in enumerate((W1_FIRST, H - W1_FIRST))
+        ]
         w23s_raw = keep.tile([P, 2, H], U8, name="w23s_raw", align_bytes=64)
-        xs_plane = keep.tile([P, S], U8, name="xs_plane", align_bytes=64)
+        xs_plane = [keep.tile([P, 2, GATHER], U8, name="xs_plane%d" % g, align_bytes=64) for g in range(V // GATHER)]
         w23s = keep.tile([P, 2, PACK, P], U8, name="w23s", align_bytes=64)
 
         nc.vector.memset(xs_table[:].bitcast(I32), 0)
         nc.gpsimd.memset(w23s_raw[:].rearrange("p w c -> p (w c)").bitcast(I32), 0)
-        nc.gpsimd.memset(xs_plane[:].bitcast(I32), 0)
+        for plane in xs_plane:
+            nc.gpsimd.memset(plane[:].rearrange("p d v -> p (d v)").bitcast(I32), 0)
         nc.gpsimd.memset(w23s[:].rearrange("p w t m -> p (w t m)").bitcast(I32), 0)
 
         nc.sync.dma_start(offsets[:], offs)
         w1_rows = w1.rearrange("(p j) c -> p j c", j=PACK)
-        for h in range(2):
-            nc.sync.dma_start(out=w1_raw[h][:], in_=w1_rows[:, :, h * (H // 2) : (h + 1) * (H // 2)])
-        nc.sync.dma_start(out=x_table[:], in_=x_words[0].rearrange("p c r -> p (c r)").bitcast(I32))
-        nc.scalar.dma_start(out=xs_table[0:P:SPREAD, :].bitcast(I32), in_=x_scales[0].bitcast(I32))
+        for rows in (slice(0, 1), slice(1, 2)):
+            nc.sync.dma_start(out=w1_raw[0][:, rows, :], in_=w1_rows[:, rows, 0:W1_FIRST])
         for w, scales in enumerate((w2_scales, w3_scales)):
-            nc.scalar.dma_start(out=w23s_raw[0:P:SPREAD, w, :].bitcast(I32), in_=scales[0].bitcast(I32))
-
-        xs_picked = keep.tile([P, S], U8, name="xs_picked", align_bytes=64)
-        nc.vector.tensor_copy(xs_picked[:], xs_table[:].indirect(offsets[:]))
-        place_scale_rows(nc.sync, xs_plane[:], xs_picked[:])
+            nc.sync.dma_start(out=w23s_raw[0:P:SPREAD, w, :].bitcast(I32), in_=scales[0].bitcast(I32))
+        nc.sync.dma_start(out=w1_raw[0][:, 2:PACK, :], in_=w1_rows[:, 2:PACK, 0:W1_FIRST])
+        nc.sync.dma_start(out=xs_table[0:P:SPREAD, :].bitcast(I32), in_=x_scales[0].bitcast(I32))
+        nc.sync.dma_start(out=w1_raw[1][:], in_=w1_rows[:, :, W1_FIRST:H])
+        nc.sync.dma_start(out=x_table[:], in_=x_words[0].rearrange("p c r -> p (c r)").bitcast(I32))
 
         w23s_dealt = keep.tile([P, 2, PACK, P], U8, name="w23s_dealt", align_bytes=64)
         nc.vector.tensor_copy(out=w23s_dealt[:], in_=w23s_raw[:].rearrange("p w (m t) -> p w t m", t=PACK))
+
+        for g in range(V // GATHER):
+            xs_picked = keep.tile([P, 2, GATHER], U8, name="xs_picked%d" % g, align_bytes=64)
+            for d in (1, 0):
+                first = d * V + g * GATHER
+                nc.vector.tensor_copy(
+                    xs_picked[:, d, :],
+                    xs_table[:].indirect(offsets[:, first // LIST_ROWS : (first + GATHER) // LIST_ROWS]),
+                )
+            place_scale_rows(
+                nc.sync, xs_plane[g][:].rearrange("p d v -> p (d v)"), xs_picked[:].rearrange("p d v -> p (d v)")
+            )
 
         w23_raw = keep.tile([P, 2, 2 * H], U8, name="w23_raw", tag="xs_table", align_bytes=64)
         for w, words in enumerate((w2_words, w3_words)):
             nc.sync.dma_start(out=w23_raw[:, w, :].bitcast(I32), in_=words[0].bitcast(I32))
         place_scale_rows(
-            nc.sync, w23s[:].rearrange("p w t m -> p (w t m)"), w23s_dealt[:].rearrange("p w t m -> p (w t m)")
+            nc.gpsimd, w23s[:].rearrange("p w t m -> p (w t m)"), w23s_dealt[:].rearrange("p w t m -> p (w t m)")
         )
 
         w1_bf = keep.tile([P, PACK, P, PACK], BF16, name="w1_bf", tag="w1_bf", align_bytes=64)
-        for h in range(2):
+        for h, rows in ((0, slice(0, 1)), (0, slice(1, PACK)), (1, slice(0, PACK))):
+            groups = slice(0, W1_FIRST // PACK) if h == 0 else slice(W1_FIRST // PACK, P)
             nc.scalar.activation(
-                out=w1_bf[:, :, h * (P // 2) : (h + 1) * (P // 2), :].rearrange("p t m j -> p m t j"),
-                in_=w1_raw[h][:].rearrange("p j (m t) -> p m t j", t=PACK),
+                out=w1_bf[:, :, groups, rows].rearrange("p t m j -> p m t j"),
+                in_=w1_raw[h][:, rows, :].rearrange("p j (m t) -> p m t j", t=PACK),
                 func=ACT.Copy,
                 scale=0.5,
             )
@@ -123,7 +139,7 @@ def tile_picked_haar_relu_po_kernel(
                         lhsT=w1_codes[:, t * P : (t + 1) * P].bitcast(FP8X4),
                         lhsT_scale=w1_scales[:, t * P : (t + 1) * P],
                         rhs=x_picked[:, d * V + first : d * V + first + CHUNK].bitcast(FP8X4),
-                        rhs_scale=xs_plane[:, d * V + first : d * V + first + CHUNK],
+                        rhs_scale=xs_plane[first // GATHER][:, d, first % GATHER : first % GATHER + CHUNK],
                         start=True,
                         stop=True,
                     )

@@ -53,11 +53,11 @@ def tile_picked_haar_relu_po_kernel(
         xs_plane = [keep.tile([P, 2, GATHER], U8, name="xs_plane%d" % g, align_bytes=64) for g in range(V // GATHER)]
         w23s = keep.tile([P, 2, PACK, P], U8, name="w23s", align_bytes=64)
 
+        nc.vector.memset(w23s_raw[:].rearrange("p w c -> p (w c)").bitcast(I32), 0)
         nc.vector.memset(xs_table[:].bitcast(I32), 0)
-        nc.gpsimd.memset(w23s_raw[:].rearrange("p w c -> p (w c)").bitcast(I32), 0)
         for plane in xs_plane:
-            nc.gpsimd.memset(plane[:].rearrange("p d v -> p (d v)").bitcast(I32), 0)
-        nc.gpsimd.memset(w23s[:].rearrange("p w t m -> p (w t m)").bitcast(I32), 0)
+            nc.vector.memset(plane[:].rearrange("p d v -> p (d v)").bitcast(I32), 0)
+        nc.vector.memset(w23s[:].rearrange("p w t m -> p (w t m)").bitcast(I32), 0)
 
         nc.sync.dma_start(offsets[:], offs)
         w1_rows = w1.rearrange("(p j) c -> p j c", j=PACK)
@@ -96,8 +96,8 @@ def tile_picked_haar_relu_po_kernel(
         for h, rows in ((0, slice(0, 1)), (0, slice(1, PACK)), (1, slice(0, PACK))):
             groups = slice(0, W1_FIRST // PACK) if h == 0 else slice(W1_FIRST // PACK, P)
             nc.scalar.activation(
-                out=w1_bf[:, :, groups, rows].rearrange("p t m j -> p m t j"),
-                in_=w1_raw[h][:, rows, :].rearrange("p j (m t) -> p m t j", t=PACK),
+                out=w1_bf[:, :, groups, rows].rearrange("p t m j -> p m j t"),
+                in_=w1_raw[h][:, rows, :].rearrange("p j (m t) -> p m j t", t=PACK),
                 func=ACT.Copy,
                 scale=0.5,
             )
@@ -107,7 +107,7 @@ def tile_picked_haar_relu_po_kernel(
             out=w1_codes[:].bitcast(FP8X4), scales=w1_scales[:], in_=w1_bf[:].rearrange("p t m j -> p (t m j)")
         )
 
-        x_picked = keep.tile([P, S], U32, name="x_picked", tag="w1_bf", align_bytes=64)
+        x_picked = keep.tile([P, S], U32, name="x_picked", align_bytes=64)
         for g in range(V // GATHER):
             for d in (1, 0):
                 first = d * V + g * GATHER
@@ -159,26 +159,29 @@ def tile_picked_haar_relu_po_kernel(
                 op1=(ALU.add, ALU.subtract)[w],
             )
 
-        def second_product(c, band_bf):
-            band_codes = ring.tile([P, 2, CHUNK], U32, name="band_codes", align_bytes=64, bufs=4)
-            band_scales = ring.tile([P, 2, CHUNK], U8, name="band_scales", align_bytes=64, bufs=4)
+        def quantise_band(c, w):
             nc.vector.quantize_mx(
-                out=band_codes[:].rearrange("p w v -> p (w v)").bitcast(FP8X4),
-                scales=band_scales[:].rearrange("p w v -> p (w v)"),
-                in_=band_bf[:].rearrange("p w v t -> p (w v t)"),
+                out=band_codes[c][w][:].bitcast(FP8X4),
+                scales=band_scales[c][w][:],
+                in_=band_bf[c][:, w, :, :].rearrange("p v t -> p (v t)"),
             )
+
+        def second_pass(out, c, w, t):
+            nc.tensor.matmul_mx(
+                out=out,
+                lhsT=w23[:, w, t, :].bitcast(FP4X4),
+                lhsT_scale=w23s[:, w, t, :],
+                rhs=band_codes[c][w][:].bitcast(FP8X4),
+                rhs_scale=band_scales[c][w][:],
+                start=(w == 0),
+                stop=(w == 1),
+            )
+
+        def second_product(c):
             bank = psum.tile([P, PACK, CHUNK], F32, name="y_bank", bufs=2)
             for t in range(PACK):
                 for w in range(2):
-                    nc.tensor.matmul_mx(
-                        out=bank[:, t, :],
-                        lhsT=w23[:, w, t, :].bitcast(FP4X4),
-                        lhsT_scale=w23s[:, w, t, :],
-                        rhs=band_codes[:, w, :].bitcast(FP8X4),
-                        rhs_scale=band_scales[:, w, :],
-                        start=(w == 0),
-                        stop=(w == 1),
-                    )
+                    second_pass(bank[:, t, :], c, w, t)
             cols = slice(c * CHUNK, (c + 1) * CHUNK)
             y_f32 = ring.tile([P, PACK, CHUNK], F32, name="y_f32", bufs=4)
             nc.scalar.copy(out=y_f32[:], in_=bank[:])
@@ -194,29 +197,17 @@ def tile_picked_haar_relu_po_kernel(
                 in_=y_f32[:].rearrange("p t (u i) -> p u t i", i=PACK),
             )
 
-        def last_second_product(band_bf, y_before):
+        def last_second_product(y_before):
             cols = slice(V - CHUNK, V)
             banks = [
                 psum.tile([P, PACK, CHUNK], F32, name="h_bank%d" % d, bufs=3)[:, 0, :] for d in (1, 0, 1, 0)
             ]
             for w in range(2):
-                codes = keep.tile([P, CHUNK], U32, name="last_codes%d" % w, align_bytes=64)
-                scales = keep.tile([P, CHUNK], U8, name="last_scales%d" % w, align_bytes=64)
-                nc.vector.quantize_mx(
-                    out=codes[:].bitcast(FP8X4), scales=scales[:], in_=band_bf[:, w, :, :].rearrange("p v t -> p (v t)")
-                )
+                quantise_band(CHUNKS - 1, w)
                 for t in range(PACK):
-                    nc.tensor.matmul_mx(
-                        out=banks[t],
-                        lhsT=w23[:, w, t, :].bitcast(FP4X4),
-                        lhsT_scale=w23s[:, w, t, :],
-                        rhs=codes[:].bitcast(FP8X4),
-                        rhs_scale=scales[:],
-                        start=(w == 0),
-                        stop=(w == 1),
-                    )
+                    second_pass(banks[t], CHUNKS - 1, w, t)
                 if w == 0:
-                    band(1, hidden[CHUNKS - 1], band_bf)
+                    band(1, hidden[CHUNKS - 1], band_bf[CHUNKS - 1])
                     planes(slice(0, CHUNK))
             planes(slice(CHUNK, 2 * CHUNK))
             round_from_sbuf(CHUNKS - 2, y_before)
@@ -224,7 +215,7 @@ def tile_picked_haar_relu_po_kernel(
             store_codes(slice(0, 3 * CHUNK))
             y_f32 = ring.tile([P, PACK, CHUNK], F32, name="y_f32", bufs=4)
             for t in range(PACK):
-                if t < 2:
+                if t >= 2:
                     nc.scalar.copy(out=y_f32[:, t, :], in_=banks[t])
                 else:
                     nc.vector.tensor_copy(out=y_f32[:, t, :], in_=banks[t])
@@ -248,17 +239,30 @@ def tile_picked_haar_relu_po_kernel(
         band_bf = [
             ring.tile([P, 2, CHUNK, PACK], BF16, name="band_bf", align_bytes=64, bufs=4) for c in range(CHUNKS)
         ]
+        band_codes = [
+            [keep.tile([P, CHUNK], U32, name="band_codes%d_%d" % (c, w), align_bytes=64) for w in range(2)]
+            for c in range(CHUNKS)
+        ]
+        band_scales = [
+            [keep.tile([P, CHUNK], U8, name="band_scales%d_%d" % (c, w), align_bytes=64) for w in range(2)]
+            for c in range(CHUNKS)
+        ]
         for c in range(CHUNKS):
             band(0, hidden[c], band_bf[c])
             if c > 0:
-                y_bank, y_f32 = second_product(c - 1, band_bf[c - 1])
+                if c == 1:
+                    quantise_band(0, 0)
+                quantise_band(c - 1, 1)
+                y_bank, y_f32 = second_product(c - 1)
                 if c + 1 < CHUNKS:
                     round_from_bank(c - 1, y_bank)
             if c + 1 < CHUNKS:
                 band(1, hidden[c], band_bf[c])
+                if c > 0:
+                    quantise_band(c, 0)
             if c + 3 < CHUNKS:
                 hidden.append(first_product(c + 3))
-        last_second_product(band_bf[CHUNKS - 1], y_f32)
+        last_second_product(y_f32)
         for q in range(4):
             queue = nc.sync if q < 2 else nc.scalar
             queue.dma_start(

@@ -69,6 +69,9 @@ def tile_picked_haar_relu_po_kernel(
         nc.sync.dma_start(out=xs_table[0:P:SPREAD, :].bitcast(I32), in_=x_scales[0].bitcast(I32))
         nc.sync.dma_start(out=w1_raw[1][:], in_=w1_rows[:, :, W1_FIRST:H])
         nc.sync.dma_start(out=x_table[:], in_=x_words[0].rearrange("p c r -> p (c r)").bitcast(I32))
+        w23_raw = keep.tile([P, 2, 2 * H], U8, name="w23_raw", align_bytes=64)
+        for w, words in enumerate((w2_words, w3_words)):
+            nc.sync.dma_start(out=w23_raw[:, w, :].bitcast(I32), in_=words[0].bitcast(I32))
 
         w23s_dealt = keep.tile([P, 2, PACK, P], U8, name="w23s_dealt", align_bytes=64)
         nc.vector.tensor_copy(out=w23s_dealt[:], in_=w23s_raw[:].rearrange("p w (m t) -> p w t m", t=PACK))
@@ -85,9 +88,6 @@ def tile_picked_haar_relu_po_kernel(
                 nc.sync, xs_plane[g][:].rearrange("p d v -> p (d v)"), xs_picked[:].rearrange("p d v -> p (d v)")
             )
 
-        w23_raw = keep.tile([P, 2, 2 * H], U8, name="w23_raw", tag="xs_table", align_bytes=64)
-        for w, words in enumerate((w2_words, w3_words)):
-            nc.sync.dma_start(out=w23_raw[:, w, :].bitcast(I32), in_=words[0].bitcast(I32))
         place_scale_rows(
             nc.gpsimd, w23s[:].rearrange("p w t m -> p (w t m)"), w23s_dealt[:].rearrange("p w t m -> p (w t m)")
         )
@@ -210,9 +210,9 @@ def tile_picked_haar_relu_po_kernel(
                     band(1, hidden[CHUNKS - 1], band_bf[CHUNKS - 1])
                     planes(slice(0, CHUNK))
             planes(slice(CHUNK, 2 * CHUNK))
+            store_codes(slice(0, 2 * CHUNK))
             round_from_sbuf(CHUNKS - 2, y_before)
             planes(slice(2 * CHUNK, 3 * CHUNK))
-            store_codes(slice(0, 3 * CHUNK))
             y_f32 = ring.tile([P, PACK, CHUNK], F32, name="y_f32", bufs=4)
             for t in range(PACK):
                 if t >= 2:
@@ -222,7 +222,7 @@ def tile_picked_haar_relu_po_kernel(
             nc.scalar.dma_start(out=y_rows[:, :, cols], in_=y_f32[:])
             round_from_sbuf(CHUNKS - 1, y_f32)
             planes(cols)
-            store_codes(cols)
+            store_codes(slice(2 * CHUNK, V))
 
         def planes(cols):
             nc.vector.quantize_mx(

@@ -23,7 +23,11 @@ CHUNKS = V // CHUNK
 GATHER = 256
 LIST_ROWS = 16
 SPREAD = 8
-W1_FIRST = 256
+W1_HALF = 256
+W1_LATE = 128
+WARM_UPS = 3
+WARM_PAD = 448
+W1_SHARE = 64
 
 
 def place_scale_rows(queue, plane, spread):
@@ -46,77 +50,110 @@ def tile_picked_haar_relu_po_kernel(
         x_table = keep.tile([P, T], I32, name="x_table", tag="x_table", align_bytes=64)
         xs_table = keep.tile([P, T], U8, name="xs_table", tag="xs_table", align_bytes=64)
         w1_raw = [
-            keep.tile([P, PACK, width], F32, name="w1_raw%d" % h, align_bytes=64)
-            for h, width in enumerate((W1_FIRST, H - W1_FIRST))
+            keep.tile([P, PACK, width], F32, name="w1_raw%d" % h, tag="w1_raw%d" % h, align_bytes=64)
+            for h, width in enumerate((W1_HALF, W1_LATE, W1_LATE))
         ]
         w23s_raw = keep.tile([P, 2, H], U8, name="w23s_raw", align_bytes=64)
-        xs_plane = [keep.tile([P, 2, GATHER], U8, name="xs_plane%d" % g, align_bytes=64) for g in range(V // GATHER)]
+        xs_plane = keep.tile([P, S], U8, name="xs_plane", align_bytes=64)
         w23s = keep.tile([P, 2, PACK, P], U8, name="w23s", align_bytes=64)
 
-        nc.vector.memset(w23s_raw[:].rearrange("p w c -> p (w c)").bitcast(I32), 0)
         nc.vector.memset(xs_table[:].bitcast(I32), 0)
-        for plane in xs_plane:
-            nc.vector.memset(plane[:].rearrange("p d v -> p (d v)").bitcast(I32), 0)
+        nc.gpsimd.memset(w23s_raw[:].rearrange("p w c -> p (w c)").bitcast(I32), 0)
+        nc.vector.memset(xs_plane[:].bitcast(I32), 0)
         nc.vector.memset(w23s[:].rearrange("p w t m -> p (w t m)").bitcast(I32), 0)
 
         nc.sync.dma_start(offsets[:], offs)
         w1_rows = w1.rearrange("(p j) c -> p j c", j=PACK)
         for rows in (slice(0, 1), slice(1, 2)):
-            nc.sync.dma_start(out=w1_raw[0][:, rows, :], in_=w1_rows[:, rows, 0:W1_FIRST])
+            nc.sync.dma_start(out=w1_raw[0][:, rows, :], in_=w1_rows[:, rows, 0:W1_HALF])
+        nc.sync.dma_start(out=xs_table[0:P:SPREAD, :].bitcast(I32), in_=x_scales[0].bitcast(I32))
         for w, scales in enumerate((w2_scales, w3_scales)):
             nc.sync.dma_start(out=w23s_raw[0:P:SPREAD, w, :].bitcast(I32), in_=scales[0].bitcast(I32))
-        nc.sync.dma_start(out=w1_raw[0][:, 2:PACK, :], in_=w1_rows[:, 2:PACK, 0:W1_FIRST])
-        nc.sync.dma_start(out=xs_table[0:P:SPREAD, :].bitcast(I32), in_=x_scales[0].bitcast(I32))
-        nc.sync.dma_start(out=w1_raw[1][:], in_=w1_rows[:, :, W1_FIRST:H])
+        nc.sync.dma_start(out=w1_raw[0][:, 2:PACK, :], in_=w1_rows[:, 2:PACK, 0:W1_HALF])
         nc.sync.dma_start(out=x_table[:], in_=x_words[0].rearrange("p c r -> p (c r)").bitcast(I32))
+        for h in (1, 2):
+            first = W1_HALF + (h - 1) * W1_LATE
+            nc.sync.dma_start(out=w1_raw[h][:], in_=w1_rows[:, :, first : first + W1_LATE])
         w23_raw = keep.tile([P, 2, 2 * H], U8, name="w23_raw", align_bytes=64)
         for w, words in enumerate((w2_words, w3_words)):
             nc.sync.dma_start(out=w23_raw[:, w, :].bitcast(I32), in_=words[0].bitcast(I32))
 
-        w23s_dealt = keep.tile([P, 2, PACK, P], U8, name="w23s_dealt", align_bytes=64)
-        nc.vector.tensor_copy(out=w23s_dealt[:], in_=w23s_raw[:].rearrange("p w (m t) -> p w t m", t=PACK))
+        xs_picked = keep.tile([P, S], U8, name="xs_picked", align_bytes=64)
+        nc.vector.tensor_copy(xs_picked[:], xs_table[:].indirect(offsets[:]))
+        place_scale_rows(nc.sync, xs_plane[:], xs_picked[:])
 
-        for g in range(V // GATHER):
-            xs_picked = keep.tile([P, 2, GATHER], U8, name="xs_picked%d" % g, align_bytes=64)
-            for d in (1, 0):
-                first = d * V + g * GATHER
-                nc.vector.tensor_copy(
-                    xs_picked[:, d, :],
-                    xs_table[:].indirect(offsets[:, first // LIST_ROWS : (first + GATHER) // LIST_ROWS]),
-                )
-            place_scale_rows(
-                nc.sync, xs_plane[g][:].rearrange("p d v -> p (d v)"), xs_picked[:].rearrange("p d v -> p (d v)")
-            )
-
+        w23s_dealt = keep.tile([P, 2, PACK, P], U8, name="w23s_dealt", tag="xs_table", align_bytes=64)
+        nc.gpsimd.tensor_copy(out=w23s_dealt[:], in_=w23s_raw[:].rearrange("p w (m t) -> p w t m", t=PACK))
         place_scale_rows(
-            nc.gpsimd, w23s[:].rearrange("p w t m -> p (w t m)"), w23s_dealt[:].rearrange("p w t m -> p (w t m)")
+            nc.sync, w23s[:].rearrange("p w t m -> p (w t m)"), w23s_dealt[:].rearrange("p w t m -> p (w t m)")
         )
 
-        w1_bf = keep.tile([P, PACK, P, PACK], BF16, name="w1_bf", tag="w1_bf", align_bytes=64)
-        for h, rows in ((0, slice(0, 1)), (0, slice(1, PACK)), (1, slice(0, PACK))):
-            groups = slice(0, W1_FIRST // PACK) if h == 0 else slice(W1_FIRST // PACK, P)
+        w1_bf = [
+            keep.tile([P, PACK, P // 2, PACK], BF16, name="w1_bf%d" % half, tag="w1_bf%d" % half, align_bytes=64)
+            for half in range(2)
+        ]
+        padded_codes = keep.tile([P, WARM_PAD + H], U32, name="padded_codes", align_bytes=64)
+        padded_scales = keep.tile([P, WARM_PAD + H], U8, name="padded_scales", align_bytes=64)
+        nc.vector.memset(padded_codes[:, 0:WARM_PAD], 0)
+        nc.vector.memset(padded_scales[:, 0:WARM_PAD].bitcast(I32), 0)
+        w1_codes = padded_codes[:, WARM_PAD:].rearrange("p (t m) -> p t m", t=PACK)
+        w1_scales = padded_scales[:, WARM_PAD:].rearrange("p (t m) -> p t m", t=PACK)
+
+        def round_w1(raw, half, groups, rows):
             nc.scalar.activation(
-                out=w1_bf[:, :, groups, rows].rearrange("p t m j -> p m j t"),
-                in_=w1_raw[h][:, rows, :].rearrange("p j (m t) -> p m j t", t=PACK),
+                out=w1_bf[half][:, :, groups, rows].rearrange("p t m j -> p m j t"),
+                in_=raw[:, rows, :].rearrange("p j (m t) -> p m j t", t=PACK),
                 func=ACT.Copy,
                 scale=0.5,
             )
-        w1_codes = keep.tile([P, H], U32, name="w1_codes", align_bytes=64)
-        w1_scales = keep.tile([P, H], U8, name="w1_scales", align_bytes=64)
-        nc.vector.quantize_mx(
-            out=w1_codes[:].bitcast(FP8X4), scales=w1_scales[:], in_=w1_bf[:].rearrange("p t m j -> p (t m j)")
-        )
 
-        x_picked = keep.tile([P, S], U32, name="x_picked", align_bytes=64)
+        def quantise_w1(half):
+            groups = slice(half * P // 2, (half + 1) * P // 2)
+            for t in range(PACK):
+                nc.vector.quantize_mx(
+                    out=w1_codes[:, t, groups].bitcast(FP8X4),
+                    scales=w1_scales[:, t, groups],
+                    in_=w1_bf[half][:, t].rearrange("p m j -> p (m j)"),
+                )
+
+        for rows in (slice(0, 1), slice(1, PACK)):
+            round_w1(w1_raw[0][:], 0, slice(0, P // 2), rows)
+        quantise_w1(0)
+        warm = psum.tile([P, PACK, CHUNK], F32, name="y_bank", bufs=2)
+        for repeat in range(WARM_UPS):
+            nc.tensor.matmul_mx(
+                out=warm[0:32].rearrange("p t v -> p (t v)"),
+                lhsT=w1_codes[:, 0, 0:32].bitcast(FP8X4),
+                lhsT_scale=w1_scales[:, 0, 0:32],
+                rhs=padded_codes[:, 0:H].bitcast(FP8X4),
+                rhs_scale=padded_scales[:, 0:H],
+                start=True,
+                stop=True,
+            )
+        round_w1(w1_raw[1][:], 1, slice(0, W1_LATE // PACK), slice(0, PACK))
+        shared = (W1_LATE + W1_SHARE) // PACK
+        round_w1(w1_raw[2][:, :, 0:W1_SHARE], 1, slice(W1_LATE // PACK, shared), slice(0, PACK))
+        nc.vector.tensor_scalar(
+            out=w1_bf[1][:, :, shared : P // 2, :].rearrange("p t m j -> p m j t"),
+            in0=w1_raw[2][:, :, W1_SHARE:W1_LATE].rearrange("p j (m t) -> p m j t", t=PACK),
+            scalar1=0.5,
+            scalar2=None,
+            op0=ALU.mult,
+        )
+        quantise_w1(1)
+
+        x_picked = []
         for g in range(V // GATHER):
+            tag = "w1_bf1" if g == 1 else "x_picked0"
+            x_picked.append(keep.tile([P, 2, GATHER], U32, name="x_picked%d" % g, tag=tag, align_bytes=64))
             for d in (1, 0):
                 first = d * V + g * GATHER
                 nc.vector.tensor_copy(
-                    x_picked[:, first : first + GATHER],
+                    x_picked[g][:, d, :],
                     x_table[:].bitcast(U32).indirect(offsets[:, first // LIST_ROWS : (first + GATHER) // LIST_ROWS]),
                 )
 
-        w23 = keep.tile([P, 2, PACK, 2 * P], U8, name="w23", tag="x_table", align_bytes=64)
+        w23 = keep.tile([P, 2, PACK, 2 * P], U8, name="w23", align_bytes=64)
         for w in range(2):
             nc.gpsimd.tensor_copy(
                 out=w23[:, w].rearrange("p t c -> p (t c)").bitcast(U16).rearrange("p (t m) -> p t m", t=PACK),
@@ -136,10 +173,10 @@ def tile_picked_haar_relu_po_kernel(
                 for t in range(PACK):
                     nc.tensor.matmul_mx(
                         out=bank[:, t, :],
-                        lhsT=w1_codes[:, t * P : (t + 1) * P].bitcast(FP8X4),
-                        lhsT_scale=w1_scales[:, t * P : (t + 1) * P],
-                        rhs=x_picked[:, d * V + first : d * V + first + CHUNK].bitcast(FP8X4),
-                        rhs_scale=xs_plane[first // GATHER][:, d, first % GATHER : first % GATHER + CHUNK],
+                        lhsT=w1_codes[:, t, :].bitcast(FP8X4),
+                        lhsT_scale=w1_scales[:, t, :],
+                        rhs=x_picked[first // GATHER][:, d, first % GATHER : first % GATHER + CHUNK].bitcast(FP8X4),
+                        rhs_scale=xs_plane[:, d * V + first : d * V + first + CHUNK],
                         start=True,
                         stop=True,
                     )

@@ -27,7 +27,6 @@ W1_HALF = 256
 W1_LATE = 128
 WARM_UPS = 3
 WARM_PAD = 448
-W1_SHARE = 64
 
 
 def place_scale_rows(queue, plane, spread):
@@ -62,15 +61,15 @@ def tile_picked_haar_relu_po_kernel(
         nc.vector.memset(xs_plane[:].bitcast(I32), 0)
         nc.vector.memset(w23s[:].rearrange("p w t m -> p (w t m)").bitcast(I32), 0)
 
-        nc.sync.dma_start(offsets[:], offs)
         w1_rows = w1.rearrange("(p j) c -> p j c", j=PACK)
         for rows in (slice(0, 1), slice(1, 2)):
             nc.sync.dma_start(out=w1_raw[0][:, rows, :], in_=w1_rows[:, rows, 0:W1_HALF])
+        nc.sync.dma_start(offsets[:], offs)
         nc.sync.dma_start(out=xs_table[0:P:SPREAD, :].bitcast(I32), in_=x_scales[0].bitcast(I32))
-        for w, scales in enumerate((w2_scales, w3_scales)):
-            nc.sync.dma_start(out=w23s_raw[0:P:SPREAD, w, :].bitcast(I32), in_=scales[0].bitcast(I32))
         nc.sync.dma_start(out=w1_raw[0][:, 2:PACK, :], in_=w1_rows[:, 2:PACK, 0:W1_HALF])
         nc.sync.dma_start(out=x_table[:], in_=x_words[0].rearrange("p c r -> p (c r)").bitcast(I32))
+        for w, scales in enumerate((w2_scales, w3_scales)):
+            nc.sync.dma_start(out=w23s_raw[0:P:SPREAD, w, :].bitcast(I32), in_=scales[0].bitcast(I32))
         for h in (1, 2):
             first = W1_HALF + (h - 1) * W1_LATE
             nc.sync.dma_start(out=w1_raw[h][:], in_=w1_rows[:, :, first : first + W1_LATE])
@@ -130,26 +129,18 @@ def tile_picked_haar_relu_po_kernel(
                 start=True,
                 stop=True,
             )
-        round_w1(w1_raw[1][:], 1, slice(0, W1_LATE // PACK), slice(0, PACK))
-        shared = (W1_LATE + W1_SHARE) // PACK
-        round_w1(w1_raw[2][:, :, 0:W1_SHARE], 1, slice(W1_LATE // PACK, shared), slice(0, PACK))
-        nc.vector.tensor_scalar(
-            out=w1_bf[1][:, :, shared : P // 2, :].rearrange("p t m j -> p m j t"),
-            in0=w1_raw[2][:, :, W1_SHARE:W1_LATE].rearrange("p j (m t) -> p m j t", t=PACK),
-            scalar1=0.5,
-            scalar2=None,
-            op0=ALU.mult,
-        )
+        for h in (1, 2):
+            round_w1(w1_raw[h][:], 1, slice((h - 1) * W1_LATE // PACK, h * W1_LATE // PACK), slice(0, PACK))
         quantise_w1(1)
 
-        x_picked = []
+        x_picked = {}
         for g in range(V // GATHER):
-            tag = "w1_bf1" if g == 1 else "x_picked0"
-            x_picked.append(keep.tile([P, 2, GATHER], U32, name="x_picked%d" % g, tag=tag, align_bytes=64))
             for d in (1, 0):
                 first = d * V + g * GATHER
+                tag = "w1_bf1" if (g, d) == (1, 0) else "x_picked%d%d" % (g, d)
+                x_picked[g, d] = keep.tile([P, GATHER], U32, name="x_picked%d%d" % (g, d), tag=tag, align_bytes=64)
                 nc.vector.tensor_copy(
-                    x_picked[g][:, d, :],
+                    x_picked[g, d][:],
                     x_table[:].bitcast(U32).indirect(offsets[:, first // LIST_ROWS : (first + GATHER) // LIST_ROWS]),
                 )
 
@@ -165,6 +156,11 @@ def tile_picked_haar_relu_po_kernel(
         y_rows = out_0.rearrange("(p t) v -> p t v", t=PACK)
         y_words = out_1[0].rearrange("p c r -> p (c r)").bitcast(I32)
 
+        def pair_parts(c):
+            if c == 0:
+                return slice(0, CHUNK // 2), slice(CHUNK // 2, CHUNK)
+            return (slice(0, CHUNK),)
+
         def first_product(c):
             banks = {}
             for d in (1, 0):
@@ -175,23 +171,26 @@ def tile_picked_haar_relu_po_kernel(
                         out=bank[:, t, :],
                         lhsT=w1_codes[:, t, :].bitcast(FP8X4),
                         lhsT_scale=w1_scales[:, t, :],
-                        rhs=x_picked[first // GATHER][:, d, first % GATHER : first % GATHER + CHUNK].bitcast(FP8X4),
+                        rhs=x_picked[first // GATHER, d][:, first % GATHER : first % GATHER + CHUNK].bitcast(FP8X4),
                         rhs_scale=xs_plane[:, d * V + first : d * V + first + CHUNK],
                         start=True,
                         stop=True,
                     )
                 banks[d] = bank
             half_b = ring.tile([P, CHUNK, PACK], F32, name="half_b", bufs=4)
-            nc.scalar.activation(out=half_b[:], in_=banks[1][:].rearrange("p t v -> p v t"), func=ACT.Relu)
+            for part in pair_parts(c):
+                nc.scalar.activation(
+                    out=half_b[:, part, :], in_=banks[1][:, :, part].rearrange("p t v -> p v t"), func=ACT.Relu
+                )
             return banks[0], half_b
 
-        def band(w, hidden, band_bf):
+        def band(w, hidden, band_bf, part=slice(0, CHUNK)):
             bank_a, half_b = hidden
             nc.vector.scalar_tensor_tensor(
-                out=band_bf[:, w, :, :],
-                in0=bank_a[:].rearrange("p t v -> p v t"),
+                out=band_bf[:, w, part, :],
+                in0=bank_a[:, :, part].rearrange("p t v -> p v t"),
                 scalar=0.0,
-                in1=half_b[:],
+                in1=half_b[:, part, :],
                 op0=ALU.max,
                 op1=(ALU.add, ALU.subtract)[w],
             )
@@ -285,7 +284,8 @@ def tile_picked_haar_relu_po_kernel(
             for c in range(CHUNKS)
         ]
         for c in range(CHUNKS):
-            band(0, hidden[c], band_bf[c])
+            for part in pair_parts(c):
+                band(0, hidden[c], band_bf[c], part)
             if c > 0:
                 if c == 1:
                     quantise_band(0, 0)

@@ -43,10 +43,11 @@ def tile_picked_haar_relu_po_kernel(
     with ExitStack() as ctx:
         keep = ctx.enter_context(tc.tile_pool(name="keep", bufs=1))
         ring = ctx.enter_context(tc.tile_pool(name="ring", bufs=2))
+        table = ctx.enter_context(tc.tile_pool(name="table", bufs=1))
         psum = ctx.enter_context(tc.psum_pool(name="psum", bufs=2))
 
         offsets = keep.tile([P, S // LIST_ROWS], U16, name="offsets")
-        x_table = keep.tile([P, T], I32, name="x_table", tag="x_table", align_bytes=64)
+        x_table = table.tile([P, T], I32, name="x_table", align_bytes=64, offset=0)
         xs_table = keep.tile([P, T], U8, name="xs_table", tag="xs_table", align_bytes=64)
         w1_raw = [
             keep.tile([P, PACK, width], F32, name="w1_raw%d" % h, tag="w1_raw%d" % h, align_bytes=64)
@@ -54,12 +55,12 @@ def tile_picked_haar_relu_po_kernel(
         ]
         w23s_raw = keep.tile([P, 2, H], U8, name="w23s_raw", align_bytes=64)
         xs_plane = keep.tile([P, S], U8, name="xs_plane", align_bytes=64)
-        w23s = keep.tile([P, 2, PACK, P], U8, name="w23s", align_bytes=64)
+        w23s_placed = keep.tile([P, 2, H], U8, name="w23s_placed", align_bytes=64)
 
         nc.vector.memset(xs_table[:].bitcast(I32), 0)
-        nc.gpsimd.memset(w23s_raw[:].rearrange("p w c -> p (w c)").bitcast(I32), 0)
+        nc.vector.memset(w23s_raw[:].rearrange("p w c -> p (w c)").bitcast(I32), 0)
         nc.vector.memset(xs_plane[:].bitcast(I32), 0)
-        nc.vector.memset(w23s[:].rearrange("p w t m -> p (w t m)").bitcast(I32), 0)
+        nc.vector.memset(w23s_placed[:].rearrange("p w c -> p (w c)").bitcast(I32), 0)
 
         w1_rows = w1.rearrange("(p j) c -> p j c", j=PACK)
         for rows in (slice(0, 1), slice(1, 2)):
@@ -81,10 +82,8 @@ def tile_picked_haar_relu_po_kernel(
         nc.vector.tensor_copy(xs_picked[:], xs_table[:].indirect(offsets[:]))
         place_scale_rows(nc.sync, xs_plane[:], xs_picked[:])
 
-        w23s_dealt = keep.tile([P, 2, PACK, P], U8, name="w23s_dealt", tag="xs_table", align_bytes=64)
-        nc.gpsimd.tensor_copy(out=w23s_dealt[:], in_=w23s_raw[:].rearrange("p w (m t) -> p w t m", t=PACK))
         place_scale_rows(
-            nc.sync, w23s[:].rearrange("p w t m -> p (w t m)"), w23s_dealt[:].rearrange("p w t m -> p (w t m)")
+            nc.sync, w23s_placed[:].rearrange("p w c -> p (w c)"), w23s_raw[:].rearrange("p w c -> p (w c)")
         )
 
         w1_bf = [
@@ -144,7 +143,9 @@ def tile_picked_haar_relu_po_kernel(
                     x_table[:].bitcast(U32).indirect(offsets[:, first // LIST_ROWS : (first + GATHER) // LIST_ROWS]),
                 )
 
-        w23 = keep.tile([P, 2, PACK, 2 * P], U8, name="w23", align_bytes=64)
+        w23 = table.tile([P, 2, PACK, 2 * P], U8, name="w23", align_bytes=64, offset=0)
+        w23s = table.tile([P, 2, PACK, P], U8, name="w23s", align_bytes=64, offset=4 * H)
+        nc.gpsimd.tensor_copy(out=w23s[:], in_=w23s_placed[:].rearrange("p w (m t) -> p w t m", t=PACK))
         for w in range(2):
             nc.gpsimd.tensor_copy(
                 out=w23[:, w].rearrange("p t c -> p (t c)").bitcast(U16).rearrange("p (t m) -> p t m", t=PACK),
@@ -286,15 +287,17 @@ def tile_picked_haar_relu_po_kernel(
         for c in range(CHUNKS):
             for part in pair_parts(c):
                 band(0, hidden[c], band_bf[c], part)
+            if c == 1:
+                band(1, hidden[c], band_bf[c])
+                quantise_band(0, 0)
             if c > 0:
-                if c == 1:
-                    quantise_band(0, 0)
                 quantise_band(c - 1, 1)
                 y_bank, y_f32 = second_product(c - 1)
                 if c + 1 < CHUNKS:
                     round_from_bank(c - 1, y_bank)
             if c + 1 < CHUNKS:
-                band(1, hidden[c], band_bf[c])
+                if c != 1:
+                    band(1, hidden[c], band_bf[c])
                 if c > 0:
                     quantise_band(c, 0)
             if c + 3 < CHUNKS:

@@ -44,7 +44,11 @@ def tile_picked_haar_relu_po_kernel(
         keep = ctx.enter_context(tc.tile_pool(name="keep", bufs=1))
         ring = ctx.enter_context(tc.tile_pool(name="ring", bufs=2))
         table = ctx.enter_context(tc.tile_pool(name="table", bufs=1))
-        psum = ctx.enter_context(tc.psum_pool(name="psum", bufs=2))
+        late = ctx.enter_context(tc.tile_pool(name="late", bufs=1))
+        psum = ctx.enter_context(tc.psum_pool(name="psum", bufs=1))
+
+        def bank_tile(number):
+            return psum.tile([P, PACK, CHUNK], F32, name="bank%d" % number, tag="bank%d" % number)
 
         offsets = keep.tile([P, S // LIST_ROWS], U16, name="offsets")
         x_table = table.tile([P, T], I32, name="x_table", align_bytes=64, offset=0)
@@ -54,12 +58,12 @@ def tile_picked_haar_relu_po_kernel(
             for h, width in enumerate((W1_HALF, W1_LATE, W1_LATE))
         ]
         w23s_raw = keep.tile([P, 2, H], U8, name="w23s_raw", align_bytes=64)
-        xs_plane = keep.tile([P, S], U8, name="xs_plane", align_bytes=64)
+        xs_plane = [keep.tile([P, 2, GATHER], U8, name="xs_plane%d" % g, align_bytes=64) for g in range(V // GATHER)]
         w23s_placed = keep.tile([P, 2, H], U8, name="w23s_placed", align_bytes=64)
 
         nc.vector.memset(xs_table[:].bitcast(I32), 0)
-        nc.vector.memset(w23s_raw[:].rearrange("p w c -> p (w c)").bitcast(I32), 0)
-        nc.vector.memset(xs_plane[:].bitcast(I32), 0)
+        for plane in xs_plane:
+            nc.vector.memset(plane[:].rearrange("p d v -> p (d v)").bitcast(I32), 0)
         nc.vector.memset(w23s_placed[:].rearrange("p w c -> p (w c)").bitcast(I32), 0)
 
         w1_rows = w1.rearrange("(p j) c -> p j c", j=PACK)
@@ -78,17 +82,25 @@ def tile_picked_haar_relu_po_kernel(
         for w, words in enumerate((w2_words, w3_words)):
             nc.sync.dma_start(out=w23_raw[:, w, :].bitcast(I32), in_=words[0].bitcast(I32))
 
-        xs_picked = keep.tile([P, S], U8, name="xs_picked", align_bytes=64)
-        nc.vector.tensor_copy(xs_picked[:], xs_table[:].indirect(offsets[:]))
-        place_scale_rows(nc.sync, xs_plane[:], xs_picked[:])
-
-        place_scale_rows(
-            nc.sync, w23s_placed[:].rearrange("p w c -> p (w c)"), w23s_raw[:].rearrange("p w c -> p (w c)")
-        )
+        for g in range(V // GATHER):
+            xs_picked = keep.tile([P, 2, GATHER], U8, name="xs_picked%d" % g, align_bytes=64)
+            for d in (1, 0):
+                first = d * V + g * GATHER
+                nc.vector.tensor_copy(
+                    xs_picked[:, d, :],
+                    xs_table[:].indirect(offsets[:, first // LIST_ROWS : (first + GATHER) // LIST_ROWS]),
+                )
+            place_scale_rows(
+                nc.sync, xs_plane[g][:].rearrange("p d v -> p (d v)"), xs_picked[:].rearrange("p d v -> p (d v)")
+            )
+            if g == 0:
+                place_scale_rows(
+                    nc.sync, w23s_placed[:].rearrange("p w c -> p (w c)"), w23s_raw[:].rearrange("p w c -> p (w c)")
+                )
 
         w1_bf = [
-            keep.tile([P, PACK, P // 2, PACK], BF16, name="w1_bf%d" % half, tag="w1_bf%d" % half, align_bytes=64)
-            for half in range(2)
+            keep.tile([P, PACK, P // 2, PACK], BF16, name="w1_bf0", align_bytes=64),
+            late.tile([P, PACK, P // 2, PACK], BF16, name="w1_bf1", align_bytes=64, offset=0),
         ]
         padded_codes = keep.tile([P, WARM_PAD + H], U32, name="padded_codes", align_bytes=64)
         padded_scales = keep.tile([P, WARM_PAD + H], U8, name="padded_scales", align_bytes=64)
@@ -117,7 +129,7 @@ def tile_picked_haar_relu_po_kernel(
         for rows in (slice(0, 1), slice(1, PACK)):
             round_w1(w1_raw[0][:], 0, slice(0, P // 2), rows)
         quantise_w1(0)
-        warm = psum.tile([P, PACK, CHUNK], F32, name="y_bank", bufs=2)
+        warm = bank_tile(6)
         for repeat in range(WARM_UPS):
             nc.tensor.matmul_mx(
                 out=warm[0:32].rearrange("p t v -> p (t v)"),
@@ -136,19 +148,24 @@ def tile_picked_haar_relu_po_kernel(
         for g in range(V // GATHER):
             for d in (1, 0):
                 first = d * V + g * GATHER
-                tag = "w1_bf1" if (g, d) == (1, 0) else "x_picked%d%d" % (g, d)
-                x_picked[g, d] = keep.tile([P, GATHER], U32, name="x_picked%d%d" % (g, d), tag=tag, align_bytes=64)
+                if (g, d) == (1, 0):
+                    x_picked[g, d] = late.tile([P, GATHER], U32, name="x_held", align_bytes=64, offset=0)
+                else:
+                    x_picked[g, d] = keep.tile([P, GATHER], U32, name="x_picked%d%d" % (g, d), align_bytes=64)
                 nc.vector.tensor_copy(
                     x_picked[g, d][:],
                     x_table[:].bitcast(U32).indirect(offsets[:, first // LIST_ROWS : (first + GATHER) // LIST_ROWS]),
                 )
 
-        w23 = table.tile([P, 2, PACK, 2 * P], U8, name="w23", align_bytes=64, offset=0)
+        w23 = [
+            table.tile([P, PACK, 2 * P], U8, name="w2_dealt", align_bytes=64, offset=0),
+            late.tile([P, PACK, 2 * P], U8, name="w3_dealt", align_bytes=64, offset=4 * GATHER),
+        ]
         w23s = table.tile([P, 2, PACK, P], U8, name="w23s", align_bytes=64, offset=4 * H)
         nc.gpsimd.tensor_copy(out=w23s[:], in_=w23s_placed[:].rearrange("p w (m t) -> p w t m", t=PACK))
-        for w in range(2):
-            nc.gpsimd.tensor_copy(
-                out=w23[:, w].rearrange("p t c -> p (t c)").bitcast(U16).rearrange("p (t m) -> p t m", t=PACK),
+        for w, engine in enumerate((nc.gpsimd, nc.vector)):
+            engine.tensor_copy(
+                out=w23[w][:].rearrange("p t c -> p (t c)").bitcast(U16).rearrange("p (t m) -> p t m", t=PACK),
                 in_=w23_raw[:, w].bitcast(U16).rearrange("p (m t) -> p t m", t=PACK),
             )
 
@@ -165,7 +182,7 @@ def tile_picked_haar_relu_po_kernel(
         def first_product(c):
             banks = {}
             for d in (1, 0):
-                bank = psum.tile([P, PACK, CHUNK], F32, name="h_bank%d" % d, bufs=3)
+                bank = bank_tile(c % 3 + 3 * (1 - d))
                 first = c * CHUNK
                 for t in range(PACK):
                     nc.tensor.matmul_mx(
@@ -173,7 +190,7 @@ def tile_picked_haar_relu_po_kernel(
                         lhsT=w1_codes[:, t, :].bitcast(FP8X4),
                         lhsT_scale=w1_scales[:, t, :],
                         rhs=x_picked[first // GATHER, d][:, first % GATHER : first % GATHER + CHUNK].bitcast(FP8X4),
-                        rhs_scale=xs_plane[:, d * V + first : d * V + first + CHUNK],
+                        rhs_scale=xs_plane[first // GATHER][:, d, first % GATHER : first % GATHER + CHUNK],
                         start=True,
                         stop=True,
                     )
@@ -206,7 +223,7 @@ def tile_picked_haar_relu_po_kernel(
         def second_pass(out, c, w, t):
             nc.tensor.matmul_mx(
                 out=out,
-                lhsT=w23[:, w, t, :].bitcast(FP4X4),
+                lhsT=w23[w][:, t, :].bitcast(FP4X4),
                 lhsT_scale=w23s[:, w, t, :],
                 rhs=band_codes[c][w][:].bitcast(FP8X4),
                 rhs_scale=band_scales[c][w][:],
@@ -215,7 +232,7 @@ def tile_picked_haar_relu_po_kernel(
             )
 
         def second_product(c):
-            bank = psum.tile([P, PACK, CHUNK], F32, name="y_bank", bufs=2)
+            bank = bank_tile((2, 0, 1)[c])
             for t in range(PACK):
                 for w in range(2):
                     second_pass(bank[:, t, :], c, w, t)
@@ -236,9 +253,7 @@ def tile_picked_haar_relu_po_kernel(
 
         def last_second_product(y_before):
             cols = slice(V - CHUNK, V)
-            banks = [
-                psum.tile([P, PACK, CHUNK], F32, name="h_bank%d" % d, bufs=3)[:, 0, :] for d in (1, 0, 1, 0)
-            ]
+            banks = [bank_tile(number)[:, 0, :] for number in (4, 5, 6, 7)]
             for w in range(2):
                 quantise_band(CHUNKS - 1, w)
                 for t in range(PACK):

@@ -23,17 +23,24 @@ CHUNKS = V // CHUNK
 GATHER = 256
 LIST_ROWS = 16
 SPREAD = 8
-W1_HALF = 256
-W1_LATE = 128
-WARM_UPS = 3
-WARM_PAD = 448
+W1_HALF = H // 2
+W1_LATE = W1_HALF // 2
+WARM_UPS = 4
+WARM_ROWS = 32
+WARM_PAD = H - P // 2
+LOW, HIGH = 0, 1
+FIRST, SECOND = 0, 1
+
+HIDDEN_BANKS = 3
+RESULT_BANKS = (2, 0, 1)
+LAST_RESULT_BANKS = (4, 5, 6, 7)
+WARM_BANK = 6
 
 
-def place_scale_rows(queue, plane, spread):
-    for q in range(4):
-        queue.dma_start(
-            out=plane[32 * q : 32 * q + 4, :].bitcast(I32), in_=spread[32 * q : 32 * q + 32 : SPREAD, :].bitcast(I32)
-        )
+def place_scale_rows(nc, plane, spread):
+    for quadrant in range(4):
+        base = 32 * quadrant
+        nc.sync.dma_start(out=plane[base : base + 4, :].bitcast(I32), in_=spread[base : base + 32 : SPREAD, :].bitcast(I32))
 
 
 def tile_picked_haar_relu_po_kernel(
@@ -52,10 +59,10 @@ def tile_picked_haar_relu_po_kernel(
 
         offsets = keep.tile([P, S // LIST_ROWS], U16, name="offsets")
         x_table = table.tile([P, T], I32, name="x_table", align_bytes=64, offset=0)
-        xs_table = keep.tile([P, T], U8, name="xs_table", tag="xs_table", align_bytes=64)
+        xs_table = keep.tile([P, T], U8, name="xs_table", align_bytes=64)
         w1_raw = [
-            keep.tile([P, PACK, width], F32, name="w1_raw%d" % h, tag="w1_raw%d" % h, align_bytes=64)
-            for h, width in enumerate((W1_HALF, W1_LATE, W1_LATE))
+            keep.tile([P, PACK, width], F32, name="w1_raw%d" % piece, align_bytes=64)
+            for piece, width in enumerate((W1_HALF, W1_LATE, W1_LATE))
         ]
         w23s_raw = keep.tile([P, 2, H], U8, name="w23s_raw", align_bytes=64)
         xs_plane = [keep.tile([P, 2, GATHER], U8, name="xs_plane%d" % g, align_bytes=64) for g in range(V // GATHER)]
@@ -72,34 +79,36 @@ def tile_picked_haar_relu_po_kernel(
         nc.sync.dma_start(offsets[:], offs)
         nc.sync.dma_start(out=xs_table[0:P:SPREAD, :].bitcast(I32), in_=x_scales[0].bitcast(I32))
         nc.sync.dma_start(out=w1_raw[0][:, 2:PACK, :], in_=w1_rows[:, 2:PACK, 0:W1_HALF])
-        nc.sync.dma_start(out=x_table[:], in_=x_words[0].rearrange("p c r -> p (c r)").bitcast(I32))
         for w, scales in enumerate((w2_scales, w3_scales)):
             nc.sync.dma_start(out=w23s_raw[0:P:SPREAD, w, :].bitcast(I32), in_=scales[0].bitcast(I32))
-        for h in (1, 2):
-            first = W1_HALF + (h - 1) * W1_LATE
-            nc.sync.dma_start(out=w1_raw[h][:], in_=w1_rows[:, :, first : first + W1_LATE])
-        w23_raw = keep.tile([P, 2, 2 * H], U8, name="w23_raw", align_bytes=64)
-        for w, words in enumerate((w2_words, w3_words)):
-            nc.sync.dma_start(out=w23_raw[:, w, :].bitcast(I32), in_=words[0].bitcast(I32))
+        nc.sync.dma_start(out=x_table[:], in_=x_words[0].rearrange("p c r -> p (c r)").bitcast(I32))
+        for piece in (1, 2):
+            column = W1_HALF + (piece - 1) * W1_LATE
+            nc.sync.dma_start(out=w1_raw[piece][:], in_=w1_rows[:, :, column : column + W1_LATE])
+        w3_raw = keep.tile([P, 2 * H], U8, name="w3_raw", align_bytes=64)
+        nc.sync.dma_start(out=w3_raw[:].bitcast(I32), in_=w3_words[0].bitcast(I32))
+
+        def entries(g, d):
+            entry = d * V + g * GATHER
+            return offsets[:, entry // LIST_ROWS : (entry + GATHER) // LIST_ROWS]
+
+        xs_picked = [
+            keep.tile([P, 2, GATHER], U8, name="xs_picked%d" % g, align_bytes=64) for g in range(V // GATHER)
+        ]
+
+        def place_picked_rows(g):
+            place_scale_rows(
+                nc, xs_plane[g][:].rearrange("p d v -> p (d v)"), xs_picked[g][:].rearrange("p d v -> p (d v)")
+            )
 
         for g in range(V // GATHER):
-            xs_picked = keep.tile([P, 2, GATHER], U8, name="xs_picked%d" % g, align_bytes=64)
-            for d in (1, 0):
-                first = d * V + g * GATHER
-                nc.vector.tensor_copy(
-                    xs_picked[:, d, :],
-                    xs_table[:].indirect(offsets[:, first // LIST_ROWS : (first + GATHER) // LIST_ROWS]),
-                )
-            place_scale_rows(
-                nc.sync, xs_plane[g][:].rearrange("p d v -> p (d v)"), xs_picked[:].rearrange("p d v -> p (d v)")
-            )
-            if g == 0:
-                place_scale_rows(
-                    nc.sync, w23s_placed[:].rearrange("p w c -> p (w c)"), w23s_raw[:].rearrange("p w c -> p (w c)")
-                )
+            for d in (SECOND, FIRST):
+                nc.vector.tensor_copy(xs_picked[g][:, d, :], xs_table[:].indirect(entries(g, d)))
+        place_picked_rows(0)
+        place_scale_rows(nc, w23s_placed[:].rearrange("p w c -> p (w c)"), w23s_raw[:].rearrange("p w c -> p (w c)"))
 
         w1_bf = [
-            keep.tile([P, PACK, P // 2, PACK], BF16, name="w1_bf0", align_bytes=64),
+            keep.tile([P, PACK, P // 2, PACK], BF16, name="w1_bf0", tag="w1_bf0", align_bytes=64),
             late.tile([P, PACK, P // 2, PACK], BF16, name="w1_bf1", align_bytes=64, offset=0),
         ]
         padded_codes = keep.tile([P, WARM_PAD + H], U32, name="padded_codes", align_bytes=64)
@@ -129,33 +138,33 @@ def tile_picked_haar_relu_po_kernel(
         for rows in (slice(0, 1), slice(1, PACK)):
             round_w1(w1_raw[0][:], 0, slice(0, P // 2), rows)
         quantise_w1(0)
-        warm = bank_tile(6)
-        for repeat in range(WARM_UPS):
+        w2_raw = keep.tile([P, 2 * H], U8, name="w2_raw", tag="w1_bf0", align_bytes=64)
+        nc.sync.dma_start(out=w2_raw[:].bitcast(I32), in_=w2_words[0].bitcast(I32))
+        place_picked_rows(1)
+        warm = bank_tile(WARM_BANK)
+        for warm_up in range(WARM_UPS):
             nc.tensor.matmul_mx(
-                out=warm[0:32].rearrange("p t v -> p (t v)"),
-                lhsT=w1_codes[:, 0, 0:32].bitcast(FP8X4),
-                lhsT_scale=w1_scales[:, 0, 0:32],
+                out=warm[0:WARM_ROWS].rearrange("p t v -> p (t v)"),
+                lhsT=w1_codes[:, 0, 0:WARM_ROWS].bitcast(FP8X4),
+                lhsT_scale=w1_scales[:, 0, 0:WARM_ROWS],
                 rhs=padded_codes[:, 0:H].bitcast(FP8X4),
                 rhs_scale=padded_scales[:, 0:H],
                 start=True,
                 stop=True,
             )
-        for h in (1, 2):
-            round_w1(w1_raw[h][:], 1, slice((h - 1) * W1_LATE // PACK, h * W1_LATE // PACK), slice(0, PACK))
+        for piece in (1, 2):
+            groups = slice((piece - 1) * W1_LATE // PACK, piece * W1_LATE // PACK)
+            round_w1(w1_raw[piece][:], 1, groups, slice(0, PACK))
         quantise_w1(1)
 
         x_picked = {}
         for g in range(V // GATHER):
-            for d in (1, 0):
-                first = d * V + g * GATHER
-                if (g, d) == (1, 0):
+            for d in (SECOND, FIRST):
+                if (g, d) == (V // GATHER - 1, FIRST):
                     x_picked[g, d] = late.tile([P, GATHER], U32, name="x_held", align_bytes=64, offset=0)
                 else:
                     x_picked[g, d] = keep.tile([P, GATHER], U32, name="x_picked%d%d" % (g, d), align_bytes=64)
-                nc.vector.tensor_copy(
-                    x_picked[g, d][:],
-                    x_table[:].bitcast(U32).indirect(offsets[:, first // LIST_ROWS : (first + GATHER) // LIST_ROWS]),
-                )
+                nc.vector.tensor_copy(x_picked[g, d][:], x_table[:].bitcast(U32).indirect(entries(g, d)))
 
         w23 = [
             table.tile([P, PACK, 2 * P], U8, name="w2_dealt", align_bytes=64, offset=0),
@@ -166,7 +175,7 @@ def tile_picked_haar_relu_po_kernel(
         for w, engine in enumerate((nc.gpsimd, nc.vector)):
             engine.tensor_copy(
                 out=w23[w][:].rearrange("p t c -> p (t c)").bitcast(U16).rearrange("p (t m) -> p t m", t=PACK),
-                in_=w23_raw[:, w].bitcast(U16).rearrange("p (m t) -> p t m", t=PACK),
+                in_=(w2_raw, w3_raw)[w][:].bitcast(U16).rearrange("p (m t) -> p t m", t=PACK),
             )
 
         y_codes = keep.tile([P, V], U32, name="y_codes", align_bytes=64)
@@ -174,43 +183,47 @@ def tile_picked_haar_relu_po_kernel(
         y_rows = out_0.rearrange("(p t) v -> p t v", t=PACK)
         y_words = out_1[0].rearrange("p c r -> p (c r)").bitcast(I32)
 
+        def columns(c, count=1):
+            return slice(c * CHUNK, (c + count) * CHUNK)
+
         def pair_parts(c):
             if c == 0:
                 return slice(0, CHUNK // 2), slice(CHUNK // 2, CHUNK)
             return (slice(0, CHUNK),)
 
         def first_product(c):
+            g, place = divmod(c * CHUNK, GATHER)
             banks = {}
-            for d in (1, 0):
-                bank = bank_tile(c % 3 + 3 * (1 - d))
-                first = c * CHUNK
+            for d in (SECOND, FIRST):
+                banks[d] = bank_tile(c % HIDDEN_BANKS + (HIDDEN_BANKS if d == FIRST else 0))
                 for t in range(PACK):
                     nc.tensor.matmul_mx(
-                        out=bank[:, t, :],
+                        out=banks[d][:, t, :],
                         lhsT=w1_codes[:, t, :].bitcast(FP8X4),
                         lhsT_scale=w1_scales[:, t, :],
-                        rhs=x_picked[first // GATHER, d][:, first % GATHER : first % GATHER + CHUNK].bitcast(FP8X4),
-                        rhs_scale=xs_plane[first // GATHER][:, d, first % GATHER : first % GATHER + CHUNK],
+                        rhs=x_picked[g, d][:, place : place + CHUNK].bitcast(FP8X4),
+                        rhs_scale=xs_plane[g][:, d, place : place + CHUNK],
                         start=True,
                         stop=True,
                     )
-                banks[d] = bank
-            half_b = ring.tile([P, CHUNK, PACK], F32, name="half_b", bufs=4)
+            second_relu = ring.tile([P, CHUNK, PACK], F32, name="second_relu", bufs=CHUNKS)
             for part in pair_parts(c):
                 nc.scalar.activation(
-                    out=half_b[:, part, :], in_=banks[1][:, :, part].rearrange("p t v -> p v t"), func=ACT.Relu
+                    out=second_relu[:, part, :],
+                    in_=banks[SECOND][:, :, part].rearrange("p t v -> p v t"),
+                    func=ACT.Relu,
                 )
-            return banks[0], half_b
+            return banks[FIRST], second_relu
 
-        def band(w, hidden, band_bf, part=slice(0, CHUNK)):
-            bank_a, half_b = hidden
+        def band(c, w, part=slice(0, CHUNK)):
+            first_bank, second_relu = hidden[c]
             nc.vector.scalar_tensor_tensor(
-                out=band_bf[:, w, part, :],
-                in0=bank_a[:, :, part].rearrange("p t v -> p v t"),
+                out=band_bf[c][:, w, part, :],
+                in0=first_bank[:, :, part].rearrange("p t v -> p v t"),
                 scalar=0.0,
-                in1=half_b[:, part, :],
+                in1=second_relu[:, part, :],
                 op0=ALU.max,
-                op1=(ALU.add, ALU.subtract)[w],
+                op1=ALU.add if w == LOW else ALU.subtract,
             )
 
         def quantise_band(c, w):
@@ -227,99 +240,101 @@ def tile_picked_haar_relu_po_kernel(
                 lhsT_scale=w23s[:, w, t, :],
                 rhs=band_codes[c][w][:].bitcast(FP8X4),
                 rhs_scale=band_scales[c][w][:],
-                start=(w == 0),
-                stop=(w == 1),
+                start=(w == LOW),
+                stop=(w == HIGH),
             )
 
         def second_product(c):
-            bank = bank_tile((2, 0, 1)[c])
+            bank = bank_tile(RESULT_BANKS[c])
             for t in range(PACK):
-                for w in range(2):
+                for w in (LOW, HIGH):
                     second_pass(bank[:, t, :], c, w, t)
-            cols = slice(c * CHUNK, (c + 1) * CHUNK)
-            y_f32 = ring.tile([P, PACK, CHUNK], F32, name="y_f32", bufs=4)
+            y_f32 = ring.tile([P, PACK, CHUNK], F32, name="y_f32", bufs=CHUNKS)
             nc.scalar.copy(out=y_f32[:], in_=bank[:])
-            nc.sync.dma_start(out=y_rows[:, :, cols], in_=y_f32[:])
+            nc.sync.dma_start(out=y_rows[:, :, columns(c)], in_=y_f32[:])
             return bank, y_f32
 
         def round_from_bank(c, bank):
-            nc.scalar.copy(out=y_bf[:, c * CHUNK : (c + 1) * CHUNK, :], in_=bank[:].rearrange("p t v -> p v t"))
+            nc.scalar.copy(out=y_bf[:, columns(c), :], in_=bank[:].rearrange("p t v -> p v t"))
 
         def round_from_sbuf(c, y_f32):
             nc.vector.tensor_copy(
-                out=y_bf[:, c * CHUNK : (c + 1) * CHUNK, :].rearrange("p (u i) t -> p u t i", i=PACK),
+                out=y_bf[:, columns(c), :].rearrange("p (u i) t -> p u t i", i=PACK),
                 in_=y_f32[:].rearrange("p t (u i) -> p u t i", i=PACK),
             )
 
-        def last_second_product(y_before):
-            cols = slice(V - CHUNK, V)
-            banks = [bank_tile(number)[:, 0, :] for number in (4, 5, 6, 7)]
-            for w in range(2):
-                quantise_band(CHUNKS - 1, w)
-                for t in range(PACK):
-                    second_pass(banks[t], CHUNKS - 1, w, t)
-                if w == 0:
-                    band(1, hidden[CHUNKS - 1], band_bf[CHUNKS - 1])
-                    planes(slice(0, CHUNK))
-            planes(slice(CHUNK, 2 * CHUNK))
-            store_codes(slice(0, 2 * CHUNK))
-            round_from_sbuf(CHUNKS - 2, y_before)
-            planes(slice(2 * CHUNK, 3 * CHUNK))
-            y_f32 = ring.tile([P, PACK, CHUNK], F32, name="y_f32", bufs=4)
-            for t in range(PACK):
-                if t >= 2:
-                    nc.scalar.copy(out=y_f32[:, t, :], in_=banks[t])
-                else:
-                    nc.vector.tensor_copy(out=y_f32[:, t, :], in_=banks[t])
-            nc.scalar.dma_start(out=y_rows[:, :, cols], in_=y_f32[:])
-            round_from_sbuf(CHUNKS - 1, y_f32)
-            planes(cols)
-            store_codes(slice(2 * CHUNK, V))
-
-        def planes(cols):
+        def quantise_result(c):
             nc.vector.quantize_mx(
-                out=y_codes[:, cols].bitcast(FP8X4),
-                scales=y_scales[:, cols],
-                in_=y_bf[:, cols, :].rearrange("p v t -> p (v t)"),
+                out=y_codes[:, columns(c)].bitcast(FP8X4),
+                scales=y_scales[:, columns(c)],
+                in_=y_bf[:, columns(c), :].rearrange("p v t -> p (v t)"),
             )
 
         def store_codes(cols):
             nc.sync.dma_start(out=y_words[:, cols], in_=y_codes[:, cols].bitcast(I32))
 
+        def last_chunk(y_before):
+            last = CHUNKS - 1
+            banks = [bank_tile(number)[:, 0, :] for number in LAST_RESULT_BANKS]
+            quantise_band(last, LOW)
+            for t in range(PACK):
+                second_pass(banks[t], last, LOW, t)
+            band(last, HIGH)
+            quantise_result(0)
+            quantise_band(last, HIGH)
+            for t in range(PACK):
+                second_pass(banks[t], last, HIGH, t)
+            quantise_result(1)
+            store_codes(columns(0, 2))
+            round_from_sbuf(last - 1, y_before)
+            quantise_result(last - 1)
+            y_f32 = ring.tile([P, PACK, CHUNK], F32, name="y_f32", bufs=CHUNKS)
+            for t in range(PACK):
+                if t < PACK // 2:
+                    nc.vector.tensor_copy(out=y_f32[:, t, :], in_=banks[t])
+                else:
+                    nc.scalar.copy(out=y_f32[:, t, :], in_=banks[t])
+            nc.scalar.dma_start(out=y_rows[:, :, columns(last)], in_=y_f32[:])
+            round_from_sbuf(last, y_f32)
+            quantise_result(last)
+            store_codes(columns(last - 1, 2))
+
         y_bf = keep.tile([P, V, PACK], BF16, name="y_bf", align_bytes=64)
-        hidden = [first_product(c) for c in range(3)]
+        hidden = [first_product(c) for c in range(HIDDEN_BANKS)]
         band_bf = [
-            ring.tile([P, 2, CHUNK, PACK], BF16, name="band_bf", align_bytes=64, bufs=4) for c in range(CHUNKS)
+            ring.tile([P, 2, CHUNK, PACK], BF16, name="band_bf", align_bytes=64, bufs=CHUNKS) for c in range(CHUNKS)
         ]
         band_codes = [
-            [keep.tile([P, CHUNK], U32, name="band_codes%d_%d" % (c, w), align_bytes=64) for w in range(2)]
+            [keep.tile([P, CHUNK], U32, name="band_codes%d_%d" % (c, w), align_bytes=64) for w in (LOW, HIGH)]
             for c in range(CHUNKS)
         ]
         band_scales = [
-            [keep.tile([P, CHUNK], U8, name="band_scales%d_%d" % (c, w), align_bytes=64) for w in range(2)]
+            [keep.tile([P, CHUNK], U8, name="band_scales%d_%d" % (c, w), align_bytes=64) for w in (LOW, HIGH)]
             for c in range(CHUNKS)
         ]
-        for c in range(CHUNKS):
-            for part in pair_parts(c):
-                band(0, hidden[c], band_bf[c], part)
-            if c == 1:
-                band(1, hidden[c], band_bf[c])
-                quantise_band(0, 0)
-            if c > 0:
-                quantise_band(c - 1, 1)
-                y_bank, y_f32 = second_product(c - 1)
-                if c + 1 < CHUNKS:
-                    round_from_bank(c - 1, y_bank)
-            if c + 1 < CHUNKS:
-                if c != 1:
-                    band(1, hidden[c], band_bf[c])
-                if c > 0:
-                    quantise_band(c, 0)
-            if c + 3 < CHUNKS:
-                hidden.append(first_product(c + 3))
-        last_second_product(y_f32)
-        for q in range(4):
-            queue = nc.sync if q < 2 else nc.scalar
+
+        for part in pair_parts(0):
+            band(0, LOW, part)
+        band(0, HIGH)
+        hidden.append(first_product(CHUNKS - 1))
+        band(1, LOW)
+        band(1, HIGH)
+        quantise_band(0, LOW)
+        quantise_band(0, HIGH)
+        round_from_bank(0, second_product(0)[0])
+        quantise_band(1, LOW)
+        band(2, LOW)
+        quantise_band(1, HIGH)
+        round_from_bank(1, second_product(1)[0])
+        band(2, HIGH)
+        quantise_band(2, LOW)
+        band(3, LOW)
+        quantise_band(2, HIGH)
+        last_chunk(second_product(2)[1])
+
+        for quadrant in range(4):
+            queue = nc.sync if quadrant < 2 else nc.scalar
             queue.dma_start(
-                out=out_2[0, 4 * q : 4 * q + 4, :].bitcast(I32), in_=y_scales[32 * q : 32 * q + 4, :].bitcast(I32)
+                out=out_2[0, 4 * quadrant : 4 * quadrant + 4, :].bitcast(I32),
+                in_=y_scales[32 * quadrant : 32 * quadrant + 4, :].bitcast(I32),
             )

@@ -25,9 +25,9 @@ LIST_ROWS = 16
 SPREAD = 8
 W1_HALF = H // 2
 W1_LATE = W1_HALF // 2
-WARM_UPS = 4
+WARM_UPS = 5
 WARM_ROWS = 32
-WARM_PAD = H - P // 2
+WARM_WORDS = 32
 LOW, HIGH = 0, 1
 FIRST, SECOND = 0, 1
 
@@ -92,6 +92,20 @@ def tile_picked_haar_relu_po_kernel(
             entry = d * V + g * GATHER
             return offsets[:, entry // LIST_ROWS : (entry + GATHER) // LIST_ROWS]
 
+        warm_bf = keep.tile([P, PACK * WARM_WORDS], BF16, name="warm_bf", align_bytes=64)
+        warm_source = keep.tile([P, WARM_WORDS], U32, name="warm_source", align_bytes=64)
+        warm_source_scales = keep.tile([P, WARM_WORDS], U8, name="warm_source_scales", align_bytes=64)
+        repeats = H // WARM_WORDS
+        warm_codes = keep.tile([P, repeats, WARM_WORDS], U32, name="warm_codes", align_bytes=64)
+        warm_scales = keep.tile([P, repeats, WARM_WORDS], U8, name="warm_scales", align_bytes=64)
+        nc.gpsimd.tensor_copy(out=warm_bf[:], in_=w1_raw[0][:, 0, 0 : PACK * WARM_WORDS])
+        nc.vector.quantize_mx(out=warm_source[:].bitcast(FP8X4), scales=warm_source_scales[:], in_=warm_bf[:])
+        nc.scalar.copy(
+            out=warm_scales[:].bitcast(U32),
+            in_=warm_source_scales[:].bitcast(U32).unsqueeze(1).broadcast_to([P, repeats, WARM_WORDS // 4]),
+        )
+        nc.scalar.copy(out=warm_codes[:], in_=warm_source[:].unsqueeze(1).broadcast_to([P, repeats, WARM_WORDS]))
+
         xs_picked = [
             keep.tile([P, 2, GATHER], U8, name="xs_picked%d" % g, align_bytes=64) for g in range(V // GATHER)
         ]
@@ -111,12 +125,8 @@ def tile_picked_haar_relu_po_kernel(
             keep.tile([P, PACK, P // 2, PACK], BF16, name="w1_bf0", tag="w1_bf0", align_bytes=64),
             late.tile([P, PACK, P // 2, PACK], BF16, name="w1_bf1", align_bytes=64, offset=0),
         ]
-        padded_codes = keep.tile([P, WARM_PAD + H], U32, name="padded_codes", align_bytes=64)
-        padded_scales = keep.tile([P, WARM_PAD + H], U8, name="padded_scales", align_bytes=64)
-        nc.vector.memset(padded_codes[:, 0:WARM_PAD], 0)
-        nc.vector.memset(padded_scales[:, 0:WARM_PAD].bitcast(I32), 0)
-        w1_codes = padded_codes[:, WARM_PAD:].rearrange("p (t m) -> p t m", t=PACK)
-        w1_scales = padded_scales[:, WARM_PAD:].rearrange("p (t m) -> p t m", t=PACK)
+        w1_codes = keep.tile([P, PACK, P], U32, name="w1_codes", align_bytes=64)
+        w1_scales = keep.tile([P, PACK, P], U8, name="w1_scales", align_bytes=64)
 
         def round_w1(raw, half, groups, rows):
             nc.scalar.activation(
@@ -147,8 +157,8 @@ def tile_picked_haar_relu_po_kernel(
                 out=warm[0:WARM_ROWS].rearrange("p t v -> p (t v)"),
                 lhsT=w1_codes[:, 0, 0:WARM_ROWS].bitcast(FP8X4),
                 lhsT_scale=w1_scales[:, 0, 0:WARM_ROWS],
-                rhs=padded_codes[:, 0:H].bitcast(FP8X4),
-                rhs_scale=padded_scales[:, 0:H],
+                rhs=warm_codes[:].rearrange("p r m -> p (r m)").bitcast(FP8X4),
+                rhs_scale=warm_scales[:].rearrange("p r m -> p (r m)"),
                 start=True,
                 stop=True,
             )

@@ -177,16 +177,19 @@ def tile_picked_haar_relu_po_kernel(
                 nc.vector.tensor_copy(x_picked[g, d][:], x_table[:].bitcast(U32).indirect(entries(g, d)))
 
         w23 = [
-            table.tile([P, PACK, 2 * P], U8, name="w2_dealt", align_bytes=64, offset=0),
+            keep.tile([P, PACK, 2 * P], U8, name="w2_dealt", tag="x_picked0%d" % SECOND, align_bytes=64),
             late.tile([P, PACK, 2 * P], U8, name="w3_dealt", align_bytes=64, offset=4 * GATHER),
         ]
         w23s = table.tile([P, 2, PACK, P], U8, name="w23s", align_bytes=64, offset=4 * H)
         nc.gpsimd.tensor_copy(out=w23s[:], in_=w23s_placed[:].rearrange("p w (m t) -> p w t m", t=PACK))
-        for w, engine in enumerate((nc.gpsimd, nc.vector)):
-            engine.tensor_copy(
+
+        def deal_words(w, copy):
+            copy(
                 out=w23[w][:].rearrange("p t c -> p (t c)").bitcast(U16).rearrange("p (t m) -> p t m", t=PACK),
                 in_=(w2_raw, w3_raw)[w][:].bitcast(U16).rearrange("p (m t) -> p t m", t=PACK),
             )
+
+        deal_words(HIGH, nc.vector.tensor_copy)
 
         y_codes = keep.tile([P, V], U32, name="y_codes", align_bytes=64)
         y_scales = keep.tile([P, V], U8, name="y_scales", align_bytes=64)
@@ -310,7 +313,9 @@ def tile_picked_haar_relu_po_kernel(
             store_codes(columns(last - 1, 2))
 
         y_bf = keep.tile([P, V, PACK], BF16, name="y_bf", align_bytes=64)
-        hidden = [first_product(c) for c in range(HIDDEN_BANKS)]
+        hidden = [first_product(0), first_product(1)]
+        deal_words(LOW, nc.scalar.copy)
+        hidden.append(first_product(2))
         band_bf = [
             ring.tile([P, 2, CHUNK, PACK], BF16, name="band_bf", align_bytes=64, bufs=CHUNKS) for c in range(CHUNKS)
         ]

@@ -100,11 +100,11 @@ def tile_picked_haar_relu_po_kernel(
         warm_scales = keep.tile([P, repeats, WARM_WORDS], U8, name="warm_scales", align_bytes=64)
         nc.gpsimd.tensor_copy(out=warm_bf[:], in_=w1_raw[0][:, 0, 0 : PACK * WARM_WORDS])
         nc.vector.quantize_mx(out=warm_source[:].bitcast(FP8X4), scales=warm_source_scales[:], in_=warm_bf[:])
-        nc.scalar.copy(
+        nc.gpsimd.tensor_copy(
             out=warm_scales[:].bitcast(U32),
             in_=warm_source_scales[:].bitcast(U32).unsqueeze(1).broadcast_to([P, repeats, WARM_WORDS // 4]),
         )
-        nc.scalar.copy(out=warm_codes[:], in_=warm_source[:].unsqueeze(1).broadcast_to([P, repeats, WARM_WORDS]))
+        nc.gpsimd.tensor_copy(out=warm_codes[:], in_=warm_source[:].unsqueeze(1).broadcast_to([P, repeats, WARM_WORDS]))
 
         xs_picked = [
             keep.tile([P, 2, GATHER], U8, name="xs_picked%d" % g, align_bytes=64) for g in range(V // GATHER)

@@ -25,7 +25,8 @@ LIST_ROWS = 16
 SPREAD = 8
 W1_HALF = H // 2
 W1_LATE = W1_HALF // 2
-WARM_UPS = 5
+EARLY_WARM_UPS = 2
+WARM_UPS = 4
 WARM_ROWS = 32
 WARM_WORDS = 32
 LOW, HIGH = 0, 1
@@ -152,11 +153,13 @@ def tile_picked_haar_relu_po_kernel(
         nc.sync.dma_start(out=w2_raw[:].bitcast(I32), in_=w2_words[0].bitcast(I32))
         place_picked_rows(1)
         warm = bank_tile(WARM_BANK)
-        for warm_up in range(WARM_UPS):
+        early = (warm_source[:], warm_source_scales[:])
+        behind = (w1_codes[:, 0, 0:WARM_ROWS], w1_scales[:, 0, 0:WARM_ROWS])
+        for codes, scales in EARLY_WARM_UPS * [early] + WARM_UPS * [behind]:
             nc.tensor.matmul_mx(
                 out=warm[0:WARM_ROWS].rearrange("p t v -> p (t v)"),
-                lhsT=w1_codes[:, 0, 0:WARM_ROWS].bitcast(FP8X4),
-                lhsT_scale=w1_scales[:, 0, 0:WARM_ROWS],
+                lhsT=codes.bitcast(FP8X4),
+                lhsT_scale=scales,
                 rhs=warm_codes[:].rearrange("p r m -> p (r m)").bitcast(FP8X4),
                 rhs_scale=warm_scales[:].rearrange("p r m -> p (r m)"),
                 start=True,
@@ -270,17 +273,17 @@ def tile_picked_haar_relu_po_kernel(
         def round_from_bank(c, bank):
             nc.scalar.copy(out=y_bf[:, columns(c), :], in_=bank[:].rearrange("p t v -> p v t"))
 
-        def round_from_sbuf(c, y_f32):
+        def round_from_sbuf(c, y_f32, part=slice(0, CHUNK)):
             nc.vector.tensor_copy(
-                out=y_bf[:, columns(c), :].rearrange("p (u i) t -> p u t i", i=PACK),
-                in_=y_f32[:].rearrange("p t (u i) -> p u t i", i=PACK),
+                out=y_bf[:, columns(c), :][:, part].rearrange("p (u i) t -> p u t i", i=PACK),
+                in_=y_f32[:, :, part].rearrange("p t (u i) -> p u t i", i=PACK),
             )
 
-        def quantise_result(c):
+        def quantise_result(c, part=slice(0, CHUNK)):
             nc.vector.quantize_mx(
-                out=y_codes[:, columns(c)].bitcast(FP8X4),
-                scales=y_scales[:, columns(c)],
-                in_=y_bf[:, columns(c), :].rearrange("p v t -> p (v t)"),
+                out=y_codes[:, columns(c)][:, part].bitcast(FP8X4),
+                scales=y_scales[:, columns(c)][:, part],
+                in_=y_bf[:, columns(c), :][:, part].rearrange("p v t -> p (v t)"),
             )
 
         def store_codes(cols):
@@ -308,8 +311,11 @@ def tile_picked_haar_relu_po_kernel(
                 else:
                     nc.scalar.copy(out=y_f32[:, t, :], in_=banks[t])
             nc.scalar.dma_start(out=y_rows[:, :, columns(last)], in_=y_f32[:])
-            round_from_sbuf(last, y_f32)
-            quantise_result(last)
+            halves = slice(0, CHUNK // 2), slice(CHUNK // 2, CHUNK)
+            for part in halves:
+                round_from_sbuf(last, y_f32, part)
+            for part in halves:
+                quantise_result(last, part)
             store_codes(columns(last - 1, 2))
 
         y_bf = keep.tile([P, V, PACK], BF16, name="y_bf", align_bytes=64)

@@ -52,6 +52,7 @@ def tile_picked_haar_relu_po_kernel(
         keep = ctx.enter_context(tc.tile_pool(name="keep", bufs=1))
         ring = ctx.enter_context(tc.tile_pool(name="ring", bufs=2))
         table = ctx.enter_context(tc.tile_pool(name="table", bufs=1))
+        early = ctx.enter_context(tc.tile_pool(name="early", bufs=1))
         late = ctx.enter_context(tc.tile_pool(name="late", bufs=1))
         psum = ctx.enter_context(tc.psum_pool(name="psum", bufs=1))
 
@@ -86,8 +87,6 @@ def tile_picked_haar_relu_po_kernel(
         for piece in (1, 2):
             column = W1_HALF + (piece - 1) * W1_LATE
             nc.sync.dma_start(out=w1_raw[piece][:], in_=w1_rows[:, :, column : column + W1_LATE])
-        w3_raw = keep.tile([P, 2 * H], U8, name="w3_raw", align_bytes=64)
-        nc.sync.dma_start(out=w3_raw[:].bitcast(I32), in_=w3_words[0].bitcast(I32))
 
         def entries(g, d):
             entry = d * V + g * GATHER
@@ -123,7 +122,7 @@ def tile_picked_haar_relu_po_kernel(
         place_scale_rows(nc, w23s_placed[:].rearrange("p w c -> p (w c)"), w23s_raw[:].rearrange("p w c -> p (w c)"))
 
         w1_bf = [
-            keep.tile([P, PACK, P // 2, PACK], BF16, name="w1_bf0", tag="w1_bf0", align_bytes=64),
+            early.tile([P, PACK, P // 2, PACK], BF16, name="w1_bf0", align_bytes=64, offset=0),
             late.tile([P, PACK, P // 2, PACK], BF16, name="w1_bf1", align_bytes=64, offset=0),
         ]
         w1_codes = keep.tile([P, PACK, P], U32, name="w1_codes", align_bytes=64)
@@ -149,8 +148,10 @@ def tile_picked_haar_relu_po_kernel(
         for rows in (slice(0, 1), slice(1, PACK)):
             round_w1(w1_raw[0][:], 0, slice(0, P // 2), rows)
         quantise_w1(0)
-        w2_raw = keep.tile([P, 2 * H], U8, name="w2_raw", tag="w1_bf0", align_bytes=64)
+        w2_raw = early.tile([P, 2 * H], U8, name="w2_raw", align_bytes=64, offset=0)
+        w3_raw = early.tile([P, 2 * H], U8, name="w3_raw", align_bytes=64, offset=2 * H)
         nc.sync.dma_start(out=w2_raw[:].bitcast(I32), in_=w2_words[0].bitcast(I32))
+        nc.sync.dma_start(out=w3_raw[:].bitcast(I32), in_=w3_words[0].bitcast(I32))
         place_picked_rows(1)
         warm = bank_tile(WARM_BANK)
         early = (warm_source[:], warm_source_scales[:])
@@ -181,7 +182,7 @@ def tile_picked_haar_relu_po_kernel(
 
         w23 = [
             keep.tile([P, PACK, 2 * P], U8, name="w2_dealt", tag="x_picked0%d" % SECOND, align_bytes=64),
-            late.tile([P, PACK, 2 * P], U8, name="w3_dealt", align_bytes=64, offset=4 * GATHER),
+            keep.tile([P, PACK, 2 * P], U8, name="w3_dealt", tag="x_picked0%d" % FIRST, align_bytes=64),
         ]
         w23s = table.tile([P, 2, PACK, P], U8, name="w23s", align_bytes=64, offset=4 * H)
         nc.gpsimd.tensor_copy(out=w23s[:], in_=w23s_placed[:].rearrange("p w (m t) -> p w t m", t=PACK))
@@ -192,7 +193,6 @@ def tile_picked_haar_relu_po_kernel(
                 in_=(w2_raw, w3_raw)[w][:].bitcast(U16).rearrange("p (m t) -> p t m", t=PACK),
             )
 
-        deal_words(HIGH, nc.vector.tensor_copy)
 
         y_codes = keep.tile([P, V], U32, name="y_codes", align_bytes=64)
         y_scales = keep.tile([P, V], U8, name="y_scales", align_bytes=64)
@@ -321,6 +321,7 @@ def tile_picked_haar_relu_po_kernel(
         y_bf = keep.tile([P, V, PACK], BF16, name="y_bf", align_bytes=64)
         hidden = [first_product(0), first_product(1)]
         deal_words(LOW, nc.scalar.copy)
+        deal_words(HIGH, nc.scalar.copy)
         hidden.append(first_product(2))
         band_bf = [
             ring.tile([P, 2, CHUNK, PACK], BF16, name="band_bf", align_bytes=64, bufs=CHUNKS) for c in range(CHUNKS)

@@ -249,22 +249,22 @@ def tile_picked_haar_relu_po_kernel(
                 in_=band_bf[c][:, w, :, :].rearrange("p v t -> p (v t)"),
             )
 
-        def second_pass(out, c, w, t):
+        def second_pass(out, c, w, t, start, stop):
             nc.tensor.matmul_mx(
                 out=out,
                 lhsT=w23[w][:, t, :].bitcast(FP4X4),
                 lhsT_scale=w23s[:, w, t, :],
                 rhs=band_codes[c][w][:].bitcast(FP8X4),
                 rhs_scale=band_scales[c][w][:],
-                start=(w == LOW),
-                stop=(w == HIGH),
+                start=start,
+                stop=stop,
             )
 
         def second_product(c):
             bank = bank_tile(RESULT_BANKS[c])
-            for t in range(PACK):
-                for w in (LOW, HIGH):
-                    second_pass(bank[:, t, :], c, w, t)
+            for w in (LOW, HIGH):
+                for t in range(PACK):
+                    second_pass(bank[:, t, :], c, w, t, (w, t) == (LOW, 0), (w, t) == (HIGH, PACK - 1))
             y_f32 = ring.tile([P, PACK, CHUNK], F32, name="y_f32", bufs=CHUNKS)
             nc.scalar.copy(out=y_f32[:], in_=bank[:])
             nc.sync.dma_start(out=y_rows[:, :, columns(c)], in_=y_f32[:])
@@ -294,12 +294,12 @@ def tile_picked_haar_relu_po_kernel(
             banks = [bank_tile(number)[:, 0, :] for number in LAST_RESULT_BANKS]
             quantise_band(last, LOW)
             for t in range(PACK):
-                second_pass(banks[t], last, LOW, t)
+                second_pass(banks[t], last, LOW, t, True, False)
             band(last, HIGH)
             quantise_result(0)
             quantise_band(last, HIGH)
             for t in range(PACK):
-                second_pass(banks[t], last, HIGH, t)
+                second_pass(banks[t], last, HIGH, t, False, True)
             quantise_result(1)
             store_codes(columns(0, 2))
             round_from_sbuf(last - 1, y_before)

@@ -25,6 +25,7 @@ LIST_ROWS = 16
 SPREAD = 8
 W1_HALF = H // 2
 W1_LATE = W1_HALF // 2
+FIRST_PART = 48
 EARLY_WARM_UPS = 2
 WARM_UPS = 4
 WARM_ROWS = 32
@@ -204,7 +205,7 @@ def tile_picked_haar_relu_po_kernel(
 
         def pair_parts(c):
             if c == 0:
-                return slice(0, CHUNK // 2), slice(CHUNK // 2, CHUNK)
+                return slice(0, FIRST_PART), slice(FIRST_PART, CHUNK)
             return (slice(0, CHUNK),)
 
         def first_product(c):
@@ -303,7 +304,6 @@ def tile_picked_haar_relu_po_kernel(
             quantise_result(1)
             store_codes(columns(0, 2))
             round_from_sbuf(last - 1, y_before)
-            quantise_result(last - 1)
             y_f32 = ring.tile([P, PACK, CHUNK], F32, name="y_f32", bufs=CHUNKS)
             for t in range(PACK):
                 if t < PACK // 2:
@@ -311,6 +311,7 @@ def tile_picked_haar_relu_po_kernel(
                 else:
                     nc.scalar.copy(out=y_f32[:, t, :], in_=banks[t])
             nc.scalar.dma_start(out=y_rows[:, :, columns(last)], in_=y_f32[:])
+            quantise_result(last - 1)
             halves = slice(0, CHUNK // 2), slice(CHUNK // 2, CHUNK)
             for part in halves:
                 round_from_sbuf(last, y_f32, part)
@@ -337,7 +338,7 @@ def tile_picked_haar_relu_po_kernel(
 
         for part in pair_parts(0):
             band(0, LOW, part)
-        band(0, HIGH)
+            band(0, HIGH, part)
         hidden.append(first_product(CHUNKS - 1))
         band(1, LOW)
         band(1, HIGH)

@@ -25,7 +25,6 @@ LIST_ROWS = 16
 SPREAD = 8
 W1_HALF = H // 2
 W1_LATE = W1_HALF // 2
-FIRST_PART = 48
 EARLY_WARM_UPS = 2
 WARM_UPS = 4
 WARM_ROWS = 32
@@ -68,13 +67,13 @@ def tile_picked_haar_relu_po_kernel(
             for piece, width in enumerate((W1_HALF, W1_LATE, W1_LATE))
         ]
         w23s_raw = keep.tile([P, 2, H], U8, name="w23s_raw", align_bytes=64)
-        xs_plane = [keep.tile([P, 2, GATHER], U8, name="xs_plane%d" % g, align_bytes=64) for g in range(V // GATHER)]
-        w23s_placed = keep.tile([P, 2, H], U8, name="w23s_placed", align_bytes=64)
+        planes = keep.tile([P, S], U8, name="planes", align_bytes=64)
+        xs_plane = [planes[:, 2 * GATHER * g : 2 * GATHER * (g + 1)] for g in range(V // GATHER)]
+        w23s_placed = keep.tile([P, 2 * H], U8, name="w23s_placed", align_bytes=64)
 
         nc.vector.memset(xs_table[:].bitcast(I32), 0)
-        for plane in xs_plane:
-            nc.vector.memset(plane[:].rearrange("p d v -> p (d v)").bitcast(I32), 0)
-        nc.vector.memset(w23s_placed[:].rearrange("p w c -> p (w c)").bitcast(I32), 0)
+        nc.vector.memset(planes[:].bitcast(I32), 0)
+        nc.vector.memset(w23s_placed[:].bitcast(I32), 0)
 
         w1_rows = w1.rearrange("(p j) c -> p j c", j=PACK)
         for rows in (slice(0, 1), slice(1, 2)):
@@ -88,6 +87,8 @@ def tile_picked_haar_relu_po_kernel(
         for piece in (1, 2):
             column = W1_HALF + (piece - 1) * W1_LATE
             nc.sync.dma_start(out=w1_raw[piece][:], in_=w1_rows[:, :, column : column + W1_LATE])
+        w3_raw = keep.tile([P, 2 * H], U8, name="w3_raw", align_bytes=64)
+        nc.sync.dma_start(out=w3_raw[:].bitcast(I32), in_=w3_words[0].bitcast(I32))
 
         def entries(g, d):
             entry = d * V + g * GATHER
@@ -113,14 +114,14 @@ def tile_picked_haar_relu_po_kernel(
 
         def place_picked_rows(g):
             place_scale_rows(
-                nc, xs_plane[g][:].rearrange("p d v -> p (d v)"), xs_picked[g][:].rearrange("p d v -> p (d v)")
+                nc, xs_plane[g], xs_picked[g][:].rearrange("p d v -> p (d v)")
             )
 
         for g in range(V // GATHER):
             for d in (SECOND, FIRST):
                 nc.vector.tensor_copy(xs_picked[g][:, d, :], xs_table[:].indirect(entries(g, d)))
         place_picked_rows(0)
-        place_scale_rows(nc, w23s_placed[:].rearrange("p w c -> p (w c)"), w23s_raw[:].rearrange("p w c -> p (w c)"))
+        place_scale_rows(nc, w23s_placed[:], w23s_raw[:].rearrange("p w c -> p (w c)"))
 
         w1_bf = [
             early.tile([P, PACK, P // 2, PACK], BF16, name="w1_bf0", align_bytes=64, offset=0),
@@ -150,14 +151,12 @@ def tile_picked_haar_relu_po_kernel(
             round_w1(w1_raw[0][:], 0, slice(0, P // 2), rows)
         quantise_w1(0)
         w2_raw = early.tile([P, 2 * H], U8, name="w2_raw", align_bytes=64, offset=0)
-        w3_raw = early.tile([P, 2 * H], U8, name="w3_raw", align_bytes=64, offset=2 * H)
         nc.sync.dma_start(out=w2_raw[:].bitcast(I32), in_=w2_words[0].bitcast(I32))
-        nc.sync.dma_start(out=w3_raw[:].bitcast(I32), in_=w3_words[0].bitcast(I32))
         place_picked_rows(1)
         warm = bank_tile(WARM_BANK)
-        early = (warm_source[:], warm_source_scales[:])
+        ahead = (warm_source[:], warm_source_scales[:])
         behind = (w1_codes[:, 0, 0:WARM_ROWS], w1_scales[:, 0, 0:WARM_ROWS])
-        for codes, scales in EARLY_WARM_UPS * [early] + WARM_UPS * [behind]:
+        for codes, scales in EARLY_WARM_UPS * [ahead] + WARM_UPS * [behind]:
             nc.tensor.matmul_mx(
                 out=warm[0:WARM_ROWS].rearrange("p t v -> p (t v)"),
                 lhsT=codes.bitcast(FP8X4),
@@ -183,10 +182,10 @@ def tile_picked_haar_relu_po_kernel(
 
         w23 = [
             keep.tile([P, PACK, 2 * P], U8, name="w2_dealt", tag="x_picked0%d" % SECOND, align_bytes=64),
-            keep.tile([P, PACK, 2 * P], U8, name="w3_dealt", tag="x_picked0%d" % FIRST, align_bytes=64),
+            late.tile([P, PACK, 2 * P], U8, name="w3_dealt", align_bytes=64, offset=4 * GATHER),
         ]
         w23s = table.tile([P, 2, PACK, P], U8, name="w23s", align_bytes=64, offset=4 * H)
-        nc.gpsimd.tensor_copy(out=w23s[:], in_=w23s_placed[:].rearrange("p w (m t) -> p w t m", t=PACK))
+        nc.gpsimd.tensor_copy(out=w23s[:], in_=w23s_placed[:].rearrange("p (w m t) -> p w t m", w=2, t=PACK))
 
         def deal_words(w, copy):
             copy(
@@ -194,6 +193,8 @@ def tile_picked_haar_relu_po_kernel(
                 in_=(w2_raw, w3_raw)[w][:].bitcast(U16).rearrange("p (m t) -> p t m", t=PACK),
             )
 
+
+        deal_words(HIGH, nc.vector.tensor_copy)
 
         y_codes = keep.tile([P, V], U32, name="y_codes", align_bytes=64)
         y_scales = keep.tile([P, V], U8, name="y_scales", align_bytes=64)
@@ -205,7 +206,7 @@ def tile_picked_haar_relu_po_kernel(
 
         def pair_parts(c):
             if c == 0:
-                return slice(0, FIRST_PART), slice(FIRST_PART, CHUNK)
+                return slice(0, CHUNK // 2), slice(CHUNK // 2, CHUNK)
             return (slice(0, CHUNK),)
 
         def first_product(c):
@@ -219,7 +220,7 @@ def tile_picked_haar_relu_po_kernel(
                         lhsT=w1_codes[:, t, :].bitcast(FP8X4),
                         lhsT_scale=w1_scales[:, t, :],
                         rhs=x_picked[g, d][:, place : place + CHUNK].bitcast(FP8X4),
-                        rhs_scale=xs_plane[g][:, d, place : place + CHUNK],
+                        rhs_scale=xs_plane[g][:, d * GATHER + place : d * GATHER + place + CHUNK],
                         start=True,
                         stop=True,
                     )
@@ -304,6 +305,7 @@ def tile_picked_haar_relu_po_kernel(
             quantise_result(1)
             store_codes(columns(0, 2))
             round_from_sbuf(last - 1, y_before)
+            quantise_result(last - 1)
             y_f32 = ring.tile([P, PACK, CHUNK], F32, name="y_f32", bufs=CHUNKS)
             for t in range(PACK):
                 if t < PACK // 2:
@@ -311,7 +313,6 @@ def tile_picked_haar_relu_po_kernel(
                 else:
                     nc.scalar.copy(out=y_f32[:, t, :], in_=banks[t])
             nc.scalar.dma_start(out=y_rows[:, :, columns(last)], in_=y_f32[:])
-            quantise_result(last - 1)
             halves = slice(0, CHUNK // 2), slice(CHUNK // 2, CHUNK)
             for part in halves:
                 round_from_sbuf(last, y_f32, part)
@@ -322,7 +323,6 @@ def tile_picked_haar_relu_po_kernel(
         y_bf = keep.tile([P, V, PACK], BF16, name="y_bf", align_bytes=64)
         hidden = [first_product(0), first_product(1)]
         deal_words(LOW, nc.scalar.copy)
-        deal_words(HIGH, nc.scalar.copy)
         hidden.append(first_product(2))
         band_bf = [
             ring.tile([P, 2, CHUNK, PACK], BF16, name="band_bf", align_bytes=64, bufs=CHUNKS) for c in range(CHUNKS)
@@ -338,7 +338,7 @@ def tile_picked_haar_relu_po_kernel(
 
         for part in pair_parts(0):
             band(0, LOW, part)
-            band(0, HIGH, part)
+        band(0, HIGH)
         hidden.append(first_product(CHUNKS - 1))
         band(1, LOW)
         band(1, HIGH)

@@ -25,8 +25,8 @@ LIST_ROWS = 16
 SPREAD = 8
 W1_HALF = H // 2
 W1_LATE = W1_HALF // 2
-EARLY_WARM_UPS = 2
-WARM_UPS = 4
+EARLY_WARM_UPS = 5
+WARM_UPS = 1
 WARM_ROWS = 32
 WARM_WORDS = 32
 LOW, HIGH = 0, 1
@@ -61,7 +61,7 @@ def tile_picked_haar_relu_po_kernel(
 
         offsets = keep.tile([P, S // LIST_ROWS], U16, name="offsets")
         x_table = table.tile([P, T], I32, name="x_table", align_bytes=64, offset=0)
-        xs_table = keep.tile([P, T], U8, name="xs_table", align_bytes=64)
+        xs_table = early.tile([P, T], U8, name="xs_table", align_bytes=64, offset=0)
         w1_raw = [
             keep.tile([P, PACK, width], F32, name="w1_raw%d" % piece, align_bytes=64)
             for piece, width in enumerate((W1_HALF, W1_LATE, W1_LATE))
@@ -80,10 +80,10 @@ def tile_picked_haar_relu_po_kernel(
             nc.sync.dma_start(out=w1_raw[0][:, rows, :], in_=w1_rows[:, rows, 0:W1_HALF])
         nc.sync.dma_start(offsets[:], offs)
         nc.sync.dma_start(out=xs_table[0:P:SPREAD, :].bitcast(I32), in_=x_scales[0].bitcast(I32))
-        nc.sync.dma_start(out=w1_raw[0][:, 2:PACK, :], in_=w1_rows[:, 2:PACK, 0:W1_HALF])
+        nc.sync.dma_start(out=x_table[:], in_=x_words[0].rearrange("p c r -> p (c r)").bitcast(I32))
         for w, scales in enumerate((w2_scales, w3_scales)):
             nc.sync.dma_start(out=w23s_raw[0:P:SPREAD, w, :].bitcast(I32), in_=scales[0].bitcast(I32))
-        nc.sync.dma_start(out=x_table[:], in_=x_words[0].rearrange("p c r -> p (c r)").bitcast(I32))
+        nc.sync.dma_start(out=w1_raw[0][:, 2:PACK, :], in_=w1_rows[:, 2:PACK, 0:W1_HALF])
         for piece in (1, 2):
             column = W1_HALF + (piece - 1) * W1_LATE
             nc.sync.dma_start(out=w1_raw[piece][:], in_=w1_rows[:, :, column : column + W1_LATE])
@@ -124,7 +124,7 @@ def tile_picked_haar_relu_po_kernel(
         place_scale_rows(nc, w23s_placed[:], w23s_raw[:].rearrange("p w c -> p (w c)"))
 
         w1_bf = [
-            early.tile([P, PACK, P // 2, PACK], BF16, name="w1_bf0", align_bytes=64, offset=0),
+            keep.tile([P, PACK, P // 2, PACK], BF16, name="w1_bf0", align_bytes=64),
             late.tile([P, PACK, P // 2, PACK], BF16, name="w1_bf1", align_bytes=64, offset=0),
         ]
         w1_codes = keep.tile([P, PACK, P], U32, name="w1_codes", align_bytes=64)
@@ -147,7 +147,7 @@ def tile_picked_haar_relu_po_kernel(
                     in_=w1_bf[half][:, t].rearrange("p m j -> p (m j)"),
                 )
 
-        for rows in (slice(0, 1), slice(1, PACK)):
+        for rows in (slice(0, 1), slice(1, 2), slice(2, PACK)):
             round_w1(w1_raw[0][:], 0, slice(0, P // 2), rows)
         quantise_w1(0)
         w2_raw = early.tile([P, 2 * H], U8, name="w2_raw", align_bytes=64, offset=0)

@@ -29,6 +29,7 @@ EARLY_WARM_UPS = 5
 WARM_UPS = 1
 WARM_ROWS = 32
 WARM_WORDS = 32
+XS_FIRST = P - 16
 LOW, HIGH = 0, 1
 FIRST, SECOND = 0, 1
 
@@ -38,10 +39,13 @@ LAST_RESULT_BANKS = (4, 5, 6, 7)
 WARM_BANK = 6
 
 
-def place_scale_rows(nc, plane, spread):
+def place_scale_rows(nc, plane, rows, first, step):
     for quadrant in range(4):
-        base = 32 * quadrant
-        nc.sync.dma_start(out=plane[base : base + 4, :].bitcast(I32), in_=spread[base : base + 32 : SPREAD, :].bitcast(I32))
+        start = first + 4 * step * quadrant
+        nc.sync.dma_start(
+            out=plane[32 * quadrant : 32 * quadrant + 4, :].bitcast(I32),
+            in_=rows[start : start + 4 * step : step, :].bitcast(I32),
+        )
 
 
 def tile_picked_haar_relu_po_kernel(
@@ -71,15 +75,15 @@ def tile_picked_haar_relu_po_kernel(
         xs_plane = [planes[:, 2 * GATHER * g : 2 * GATHER * (g + 1)] for g in range(V // GATHER)]
         w23s_placed = keep.tile([P, 2 * H], U8, name="w23s_placed", align_bytes=64)
 
-        nc.vector.memset(xs_table[:].bitcast(I32), 0)
+        nc.vector.memset(xs_table[0:XS_FIRST, :].bitcast(I32), 0)
         nc.vector.memset(planes[:].bitcast(I32), 0)
         nc.vector.memset(w23s_placed[:].bitcast(I32), 0)
 
         w1_rows = w1.rearrange("(p j) c -> p j c", j=PACK)
-        for rows in (slice(0, 1), slice(1, 2)):
-            nc.sync.dma_start(out=w1_raw[0][:, rows, :], in_=w1_rows[:, rows, 0:W1_HALF])
+        nc.sync.dma_start(out=w1_raw[0][:, 0:1, :], in_=w1_rows[:, 0:1, 0:W1_HALF])
         nc.sync.dma_start(offsets[:], offs)
-        nc.sync.dma_start(out=xs_table[0:P:SPREAD, :].bitcast(I32), in_=x_scales[0].bitcast(I32))
+        nc.sync.dma_start(out=xs_table[XS_FIRST:P, :].bitcast(I32), in_=x_scales[0].bitcast(I32))
+        nc.sync.dma_start(out=w1_raw[0][:, 1:2, :], in_=w1_rows[:, 1:2, 0:W1_HALF])
         nc.sync.dma_start(out=x_table[:], in_=x_words[0].rearrange("p c r -> p (c r)").bitcast(I32))
         for w, scales in enumerate((w2_scales, w3_scales)):
             nc.sync.dma_start(out=w23s_raw[0:P:SPREAD, w, :].bitcast(I32), in_=scales[0].bitcast(I32))
@@ -114,14 +118,14 @@ def tile_picked_haar_relu_po_kernel(
 
         def place_picked_rows(g):
             place_scale_rows(
-                nc, xs_plane[g], xs_picked[g][:].rearrange("p d v -> p (d v)")
+                nc, xs_plane[g], xs_picked[g][:].rearrange("p d v -> p (d v)"), XS_FIRST, 1
             )
 
         for g in range(V // GATHER):
             for d in (SECOND, FIRST):
                 nc.vector.tensor_copy(xs_picked[g][:, d, :], xs_table[:].indirect(entries(g, d)))
         place_picked_rows(0)
-        place_scale_rows(nc, w23s_placed[:], w23s_raw[:].rearrange("p w c -> p (w c)"))
+        place_scale_rows(nc, w23s_placed[:], w23s_raw[:].rearrange("p w c -> p (w c)"), 0, SPREAD)
 
         w1_bf = [
             keep.tile([P, PACK, P // 2, PACK], BF16, name="w1_bf0", align_bytes=64),
@@ -171,18 +175,25 @@ def tile_picked_haar_relu_po_kernel(
             round_w1(w1_raw[piece][:], 1, groups, slice(0, PACK))
         quantise_w1(1)
 
-        x_picked = {}
-        for g in range(V // GATHER):
-            for d in (SECOND, FIRST):
-                if (g, d) == (V // GATHER - 1, FIRST):
-                    x_picked[g, d] = late.tile([P, GATHER], U32, name="x_held", align_bytes=64, offset=0)
-                else:
-                    x_picked[g, d] = keep.tile([P, GATHER], U32, name="x_picked%d%d" % (g, d), align_bytes=64)
-                nc.vector.tensor_copy(x_picked[g, d][:], x_table[:].bitcast(U32).indirect(entries(g, d)))
+        pieces = ((V, 2 * CHUNK), (0, 3 * CHUNK), (V + 2 * CHUNK, 2 * CHUNK), (3 * CHUNK, CHUNK))
+        x_picked = [
+            keep.tile([P, 2 * CHUNK], U32, name="x_picked0", align_bytes=64),
+            keep.tile([P, 3 * CHUNK], U32, name="x_picked1", align_bytes=64),
+            late.tile([P, 2 * CHUNK], U32, name="x_held2", align_bytes=64, offset=0),
+            late.tile([P, CHUNK], U32, name="x_held3", align_bytes=64, offset=8 * CHUNK),
+        ]
+        for picked, (start, count) in zip(x_picked, pieces):
+            listed = offsets[:, start // LIST_ROWS : (start + count) // LIST_ROWS]
+            nc.vector.tensor_copy(picked[:], x_table[:].bitcast(U32).indirect(listed))
+
+        def picked_words(entry):
+            for picked, (start, count) in zip(x_picked, pieces):
+                if start <= entry < start + count:
+                    return picked[:, entry - start : entry - start + CHUNK]
 
         w23 = [
-            keep.tile([P, PACK, 2 * P], U8, name="w2_dealt", tag="x_picked0%d" % SECOND, align_bytes=64),
-            late.tile([P, PACK, 2 * P], U8, name="w3_dealt", align_bytes=64, offset=4 * GATHER),
+            keep.tile([P, PACK, 2 * P], U8, name="w2_dealt", tag="x_picked0", align_bytes=64),
+            keep.tile([P, PACK, 2 * P], U8, name="w3_dealt", align_bytes=64),
         ]
         w23s = table.tile([P, 2, PACK, P], U8, name="w23s", align_bytes=64, offset=4 * H)
         nc.gpsimd.tensor_copy(out=w23s[:], in_=w23s_placed[:].rearrange("p (w m t) -> p w t m", w=2, t=PACK))
@@ -194,7 +205,7 @@ def tile_picked_haar_relu_po_kernel(
             )
 
 
-        deal_words(HIGH, nc.vector.tensor_copy)
+        deal_words(HIGH, nc.scalar.copy)
 
         y_codes = keep.tile([P, V], U32, name="y_codes", align_bytes=64)
         y_scales = keep.tile([P, V], U8, name="y_scales", align_bytes=64)
@@ -219,7 +230,7 @@ def tile_picked_haar_relu_po_kernel(
                         out=banks[d][:, t, :],
                         lhsT=w1_codes[:, t, :].bitcast(FP8X4),
                         lhsT_scale=w1_scales[:, t, :],
-                        rhs=x_picked[g, d][:, place : place + CHUNK].bitcast(FP8X4),
+                        rhs=picked_words(d * V + c * CHUNK).bitcast(FP8X4),
                         rhs_scale=xs_plane[g][:, d * GATHER + place : d * GATHER + place + CHUNK],
                         start=True,
                         stop=True,

@@ -58,6 +58,7 @@ def tile_picked_haar_relu_po_kernel(
         table = ctx.enter_context(tc.tile_pool(name="table", bufs=1))
         early = ctx.enter_context(tc.tile_pool(name="early", bufs=1))
         late = ctx.enter_context(tc.tile_pool(name="late", bufs=1))
+        dealt = ctx.enter_context(tc.tile_pool(name="dealt", bufs=1))
         psum = ctx.enter_context(tc.psum_pool(name="psum", bufs=1))
 
         def bank_tile(number):
@@ -177,7 +178,7 @@ def tile_picked_haar_relu_po_kernel(
 
         pieces = ((V, 2 * CHUNK), (0, 3 * CHUNK), (V + 2 * CHUNK, 2 * CHUNK), (3 * CHUNK, CHUNK))
         x_picked = [
-            keep.tile([P, 2 * CHUNK], U32, name="x_picked0", align_bytes=64),
+            dealt.tile([P, 2 * CHUNK], U32, name="x_picked0", align_bytes=64, offset=H),
             keep.tile([P, 3 * CHUNK], U32, name="x_picked1", align_bytes=64),
             late.tile([P, 2 * CHUNK], U32, name="x_held2", align_bytes=64, offset=0),
             late.tile([P, CHUNK], U32, name="x_held3", align_bytes=64, offset=8 * CHUNK),
@@ -192,8 +193,8 @@ def tile_picked_haar_relu_po_kernel(
                     return picked[:, entry - start : entry - start + CHUNK]
 
         w23 = [
-            keep.tile([P, PACK, 2 * P], U8, name="w2_dealt", tag="x_picked0", align_bytes=64),
-            keep.tile([P, PACK, 2 * P], U8, name="w3_dealt", align_bytes=64),
+            dealt.tile([P, PACK, 2 * P], U8, name="w2_dealt", align_bytes=64, offset=0),
+            dealt.tile([P, PACK, 2 * P], U8, name="w3_dealt", align_bytes=64, offset=2 * H),
         ]
         w23s = table.tile([P, 2, PACK, P], U8, name="w23s", align_bytes=64, offset=4 * H)
         nc.gpsimd.tensor_copy(out=w23s[:], in_=w23s_placed[:].rearrange("p (w m t) -> p w t m", w=2, t=PACK))
@@ -204,8 +205,6 @@ def tile_picked_haar_relu_po_kernel(
                 in_=(w2_raw, w3_raw)[w][:].bitcast(U16).rearrange("p (m t) -> p t m", t=PACK),
             )
 
-
-        deal_words(HIGH, nc.scalar.copy)
 
         y_codes = keep.tile([P, V], U32, name="y_codes", align_bytes=64)
         y_scales = keep.tile([P, V], U8, name="y_scales", align_bytes=64)
@@ -333,7 +332,8 @@ def tile_picked_haar_relu_po_kernel(
 
         y_bf = keep.tile([P, V, PACK], BF16, name="y_bf", align_bytes=64)
         hidden = [first_product(0), first_product(1)]
-        deal_words(LOW, nc.scalar.copy)
+        for w in (HIGH, LOW):
+            deal_words(w, nc.scalar.copy)
         hidden.append(first_product(2))
         band_bf = [
             ring.tile([P, 2, CHUNK, PACK], BF16, name="band_bf", align_bytes=64, bufs=CHUNKS) for c in range(CHUNKS)

@@ -176,12 +176,11 @@ def tile_picked_haar_relu_po_kernel(
             round_w1(w1_raw[piece][:], 1, groups, slice(0, PACK))
         quantise_w1(1)
 
-        pieces = ((V, 2 * CHUNK), (0, 3 * CHUNK), (V + 2 * CHUNK, 2 * CHUNK), (3 * CHUNK, CHUNK))
+        pieces = ((V, GATHER), (0, V), (V + GATHER, GATHER))
         x_picked = [
             dealt.tile([P, 2 * CHUNK], U32, name="x_picked0", align_bytes=64, offset=H),
-            keep.tile([P, 3 * CHUNK], U32, name="x_picked1", align_bytes=64),
-            late.tile([P, 2 * CHUNK], U32, name="x_held2", align_bytes=64, offset=0),
-            late.tile([P, CHUNK], U32, name="x_held3", align_bytes=64, offset=8 * CHUNK),
+            keep.tile([P, V], U32, name="x_picked1", align_bytes=64),
+            late.tile([P, GATHER], U32, name="x_held", align_bytes=64, offset=0),
         ]
         for picked, (start, count) in zip(x_picked, pieces):
             listed = offsets[:, start // LIST_ROWS : (start + count) // LIST_ROWS]

@@ -135,10 +135,10 @@ def tile_picked_haar_relu_po_kernel(
         w1_codes = keep.tile([P, PACK, P], U32, name="w1_codes", align_bytes=64)
         w1_scales = keep.tile([P, PACK, P], U8, name="w1_scales", align_bytes=64)
 
-        def round_w1(raw, half, groups, rows):
+        def round_w1(raw, half, groups, rows, slices=slice(0, PACK)):
             nc.scalar.activation(
-                out=w1_bf[half][:, :, groups, rows].rearrange("p t m j -> p m j t"),
-                in_=raw[:, rows, :].rearrange("p j (m t) -> p m j t", t=PACK),
+                out=w1_bf[half][:, slices, groups, rows].rearrange("p t m j -> p m j t"),
+                in_=raw[:, rows, :].rearrange("p j (m t) -> p m j t", t=PACK)[:, :, :, slices],
                 func=ACT.Copy,
                 scale=0.5,
             )
@@ -171,9 +171,10 @@ def tile_picked_haar_relu_po_kernel(
                 start=True,
                 stop=True,
             )
-        for piece in (1, 2):
-            groups = slice((piece - 1) * W1_LATE // PACK, piece * W1_LATE // PACK)
-            round_w1(w1_raw[piece][:], 1, groups, slice(0, PACK))
+        late_groups = W1_LATE // PACK
+        round_w1(w1_raw[1][:], 1, slice(0, late_groups), slice(0, PACK))
+        for slices in (slice(0, 2), slice(2, PACK)):
+            round_w1(w1_raw[2][:], 1, slice(late_groups, 2 * late_groups), slice(0, PACK), slices)
         quantise_w1(1)
 
         pieces = ((V, GATHER), (0, V), (V + GATHER, GATHER))

@@ -92,8 +92,6 @@ def tile_picked_haar_relu_po_kernel(
         for piece in (1, 2):
             column = W1_HALF + (piece - 1) * W1_LATE
             nc.sync.dma_start(out=w1_raw[piece][:], in_=w1_rows[:, :, column : column + W1_LATE])
-        w3_raw = keep.tile([P, 2 * H], U8, name="w3_raw", align_bytes=64)
-        nc.sync.dma_start(out=w3_raw[:].bitcast(I32), in_=w3_words[0].bitcast(I32))
 
         def entries(g, d):
             entry = d * V + g * GATHER
@@ -157,6 +155,8 @@ def tile_picked_haar_relu_po_kernel(
         quantise_w1(0)
         w2_raw = early.tile([P, 2 * H], U8, name="w2_raw", align_bytes=64, offset=0)
         nc.sync.dma_start(out=w2_raw[:].bitcast(I32), in_=w2_words[0].bitcast(I32))
+        w3_raw = early.tile([P, 2 * H], U8, name="w3_raw", align_bytes=64, offset=2 * H)
+        nc.sync.dma_start(out=w3_raw[:].bitcast(I32), in_=w3_words[0].bitcast(I32))
         place_picked_rows(1)
         warm = bank_tile(WARM_BANK)
         ahead = (warm_source[:], warm_source_scales[:])
@@ -332,7 +332,7 @@ def tile_picked_haar_relu_po_kernel(
 
         y_bf = keep.tile([P, V, PACK], BF16, name="y_bf", align_bytes=64)
         hidden = [first_product(0), first_product(1)]
-        for w in (HIGH, LOW):
+        for w in (LOW, HIGH):
             deal_words(w, nc.scalar.copy)
         hidden.append(first_product(2))
         band_bf = [

from contextlib import ExitStack

import concourse.mybir as mybir

K, T, S, V, H = 512, 2048, 1024, 512, 512
FLOPS = 2 * K * H * S + 2 * 2 * H * H * V

F32 = mybir.dt.float32
BF16 = mybir.dt.bfloat16
I32 = mybir.dt.int32
U32 = mybir.dt.uint32
U16 = mybir.dt.uint16
U8 = mybir.dt.uint8
FP8X4 = mybir.dt.float8_e4m3fn_x4
FP4X4 = mybir.dt.float4_e2m1fn_x4
ALU = mybir.AluOpType
ACT = mybir.ActivationFunctionType

P = 128
PACK = 4
CHUNK = 128
CHUNKS = V // CHUNK
GATHER = 256
LIST_ROWS = 16
SPREAD = 8
W1_HALF = H // 2
W1_LATE = W1_HALF // 2
EARLY_WARM_UPS = 5
WARM_UPS = 1
WARM_ROWS = 32
WARM_WORDS = 32
XS_FIRST = P - 16
LOW, HIGH = 0, 1
FIRST, SECOND = 0, 1

HIDDEN_BANKS = 3
RESULT_BANKS = (2, 0, 1)
LAST_RESULT_BANKS = (4, 5, 6, 7)
WARM_BANK = 6


def place_scale_rows(nc, plane, rows, first, step):
    for quadrant in range(4):
        start = first + 4 * step * quadrant
        nc.sync.dma_start(
            out=plane[32 * quadrant : 32 * quadrant + 4, :].bitcast(I32),
            in_=rows[start : start + 4 * step : step, :].bitcast(I32),
        )


def tile_picked_haar_relu_po_kernel(
    tc, x_words, x_scales, w1, w2_words, w2_scales, w3_words, w3_scales, offs, out_0, out_1, out_2
):
    nc = tc.nc
    with ExitStack() as ctx:
        keep = ctx.enter_context(tc.tile_pool(name="keep", bufs=1))
        ring = ctx.enter_context(tc.tile_pool(name="ring", bufs=2))
        table = ctx.enter_context(tc.tile_pool(name="table", bufs=1))
        early = ctx.enter_context(tc.tile_pool(name="early", bufs=1))
        late = ctx.enter_context(tc.tile_pool(name="late", bufs=1))
        dealt = ctx.enter_context(tc.tile_pool(name="dealt", bufs=1))
        psum = ctx.enter_context(tc.psum_pool(name="psum", bufs=1))

        def bank_tile(number):
            return psum.tile([P, PACK, CHUNK], F32, name="bank%d" % number, tag="bank%d" % number)

        offsets = keep.tile([P, S // LIST_ROWS], U16, name="offsets")
        x_table = table.tile([P, T], I32, name="x_table", align_bytes=64, offset=0)
        xs_table = early.tile([P, T], U8, name="xs_table", align_bytes=64, offset=0)
        w1_raw = [
            keep.tile([P, PACK, width], F32, name="w1_raw%d" % piece, align_bytes=64)
            for piece, width in enumerate((W1_HALF, W1_LATE, W1_LATE))
        ]
        w23s_raw = keep.tile([P, 2, H], U8, name="w23s_raw", align_bytes=64)
        planes = keep.tile([P, S], U8, name="planes", align_bytes=64)
        xs_plane = [planes[:, 2 * GATHER * g : 2 * GATHER * (g + 1)] for g in range(V // GATHER)]
        w23s_placed = keep.tile([P, 2 * H], U8, name="w23s_placed", align_bytes=64)

        nc.vector.memset(xs_table[0:XS_FIRST, :].bitcast(I32), 0)
        nc.vector.memset(planes[:].bitcast(I32), 0)
        nc.vector.memset(w23s_placed[:].bitcast(I32), 0)

        w1_rows = w1.rearrange("(p j) c -> p j c", j=PACK)
        nc.sync.dma_start(out=w1_raw[0][:, 0:1, :], in_=w1_rows[:, 0:1, 0:W1_HALF])
        nc.sync.dma_start(offsets[:], offs)
        nc.sync.dma_start(out=xs_table[XS_FIRST:P, :].bitcast(I32), in_=x_scales[0].bitcast(I32))
        nc.sync.dma_start(out=w1_raw[0][:, 1:2, :], in_=w1_rows[:, 1:2, 0:W1_HALF])
        nc.sync.dma_start(out=x_table[:], in_=x_words[0].rearrange("p c r -> p (c r)").bitcast(I32))
        for w, scales in enumerate((w2_scales, w3_scales)):
            nc.sync.dma_start(out=w23s_raw[0:P:SPREAD, w, :].bitcast(I32), in_=scales[0].bitcast(I32))
        nc.sync.dma_start(out=w1_raw[0][:, 2:PACK, :], in_=w1_rows[:, 2:PACK, 0:W1_HALF])
        for piece in (1, 2):
            column = W1_HALF + (piece - 1) * W1_LATE
            nc.sync.dma_start(out=w1_raw[piece][:], in_=w1_rows[:, :, column : column + W1_LATE])

        def entries(g, d):
            entry = d * V + g * GATHER
            return offsets[:, entry // LIST_ROWS : (entry + GATHER) // LIST_ROWS]

        warm_bf = keep.tile([P, PACK * WARM_WORDS], BF16, name="warm_bf", align_bytes=64)
        warm_source = keep.tile([P, WARM_WORDS], U32, name="warm_source", align_bytes=64)
        warm_source_scales = keep.tile([P, WARM_WORDS], U8, name="warm_source_scales", align_bytes=64)
        repeats = H // WARM_WORDS
        warm_codes = keep.tile([P, repeats, WARM_WORDS], U32, name="warm_codes", align_bytes=64)
        warm_scales = keep.tile([P, repeats, WARM_WORDS], U8, name="warm_scales", align_bytes=64)
        nc.gpsimd.tensor_copy(out=warm_bf[:], in_=w1_raw[0][:, 0, 0 : PACK * WARM_WORDS])
        nc.vector.quantize_mx(out=warm_source[:].bitcast(FP8X4), scales=warm_source_scales[:], in_=warm_bf[:])
        nc.gpsimd.tensor_copy(
            out=warm_scales[:].bitcast(U32),
            in_=warm_source_scales[:].bitcast(U32).unsqueeze(1).broadcast_to([P, repeats, WARM_WORDS // 4]),
        )
        nc.gpsimd.tensor_copy(out=warm_codes[:], in_=warm_source[:].unsqueeze(1).broadcast_to([P, repeats, WARM_WORDS]))

        xs_picked = [
            keep.tile([P, 2, GATHER], U8, name="xs_picked%d" % g, align_bytes=64) for g in range(V // GATHER)
        ]

        def place_picked_rows(g):
            place_scale_rows(
                nc, xs_plane[g], xs_picked[g][:].rearrange("p d v -> p (d v)"), XS_FIRST, 1
            )

        for g in range(V // GATHER):
            for d in (SECOND, FIRST):
                nc.vector.tensor_copy(xs_picked[g][:, d, :], xs_table[:].indirect(entries(g, d)))
        place_picked_rows(0)
        place_scale_rows(nc, w23s_placed[:], w23s_raw[:].rearrange("p w c -> p (w c)"), 0, SPREAD)

        w1_bf = [
            keep.tile([P, PACK, P // 2, PACK], BF16, name="w1_bf0", align_bytes=64),
            late.tile([P, PACK, P // 2, PACK], BF16, name="w1_bf1", align_bytes=64, offset=0),
        ]
        w1_codes = keep.tile([P, PACK, P], U32, name="w1_codes", align_bytes=64)
        w1_scales = keep.tile([P, PACK, P], U8, name="w1_scales", align_bytes=64)

        def round_w1(raw, half, groups, rows, slices=slice(0, PACK)):
            nc.scalar.activation(
                out=w1_bf[half][:, slices, groups, rows].rearrange("p t m j -> p m j t"),
                in_=raw[:, rows, :].rearrange("p j (m t) -> p m j t", t=PACK)[:, :, :, slices],
                func=ACT.Copy,
                scale=0.5,
            )

        def quantise_w1(half):
            groups = slice(half * P // 2, (half + 1) * P // 2)
            for t in range(PACK):
                nc.vector.quantize_mx(
                    out=w1_codes[:, t, groups].bitcast(FP8X4),
                    scales=w1_scales[:, t, groups],
                    in_=w1_bf[half][:, t].rearrange("p m j -> p (m j)"),
                )

        for rows in (slice(0, 1), slice(1, 2), slice(2, PACK)):
            round_w1(w1_raw[0][:], 0, slice(0, P // 2), rows)
        quantise_w1(0)
        w2_raw = early.tile([P, 2 * H], U8, name="w2_raw", align_bytes=64, offset=0)
        nc.sync.dma_start(out=w2_raw[:].bitcast(I32), in_=w2_words[0].bitcast(I32))
        w3_raw = early.tile([P, 2 * H], U8, name="w3_raw", align_bytes=64, offset=2 * H)
        nc.sync.dma_start(out=w3_raw[:].bitcast(I32), in_=w3_words[0].bitcast(I32))
        place_picked_rows(1)
        warm = bank_tile(WARM_BANK)
        ahead = (warm_source[:], warm_source_scales[:])
        behind = (w1_codes[:, 0, 0:WARM_ROWS], w1_scales[:, 0, 0:WARM_ROWS])
        for codes, scales in EARLY_WARM_UPS * [ahead] + WARM_UPS * [behind]:
            nc.tensor.matmul_mx(
                out=warm[0:WARM_ROWS].rearrange("p t v -> p (t v)"),
                lhsT=codes.bitcast(FP8X4),
                lhsT_scale=scales,
                rhs=warm_codes[:].rearrange("p r m -> p (r m)").bitcast(FP8X4),
                rhs_scale=warm_scales[:].rearrange("p r m -> p (r m)"),
                start=True,
                stop=True,
            )
        late_groups = W1_LATE // PACK
        round_w1(w1_raw[1][:], 1, slice(0, late_groups), slice(0, PACK))
        for slices in (slice(0, 2), slice(2, PACK)):
            round_w1(w1_raw[2][:], 1, slice(late_groups, 2 * late_groups), slice(0, PACK), slices)
        quantise_w1(1)

        pieces = ((V, GATHER), (0, V), (V + GATHER, GATHER))
        x_picked = [
            dealt.tile([P, 2 * CHUNK], U32, name="x_picked0", align_bytes=64, offset=H),
            keep.tile([P, V], U32, name="x_picked1", align_bytes=64),
            late.tile([P, GATHER], U32, name="x_held", align_bytes=64, offset=0),
        ]
        for picked, (start, count) in zip(x_picked, pieces):
            listed = offsets[:, start // LIST_ROWS : (start + count) // LIST_ROWS]
            nc.vector.tensor_copy(picked[:], x_table[:].bitcast(U32).indirect(listed))

        def picked_words(entry):
            for picked, (start, count) in zip(x_picked, pieces):
                if start <= entry < start + count:
                    return picked[:, entry - start : entry - start + CHUNK]

        w23 = [
            dealt.tile([P, PACK, 2 * P], U8, name="w2_dealt", align_bytes=64, offset=0),
            dealt.tile([P, PACK, 2 * P], U8, name="w3_dealt", align_bytes=64, offset=2 * H),
        ]
        w23s = table.tile([P, 2, PACK, P], U8, name="w23s", align_bytes=64, offset=4 * H)
        nc.gpsimd.tensor_copy(out=w23s[:], in_=w23s_placed[:].rearrange("p (w m t) -> p w t m", w=2, t=PACK))

        def deal_words(w, copy):
            copy(
                out=w23[w][:].rearrange("p t c -> p (t c)").bitcast(U16).rearrange("p (t m) -> p t m", t=PACK),
                in_=(w2_raw, w3_raw)[w][:].bitcast(U16).rearrange("p (m t) -> p t m", t=PACK),
            )


        y_codes = keep.tile([P, V], U32, name="y_codes", align_bytes=64)
        y_scales = keep.tile([P, V], U8, name="y_scales", align_bytes=64)
        y_rows = out_0.rearrange("(p t) v -> p t v", t=PACK)
        y_words = out_1[0].rearrange("p c r -> p (c r)").bitcast(I32)

        def columns(c, count=1):
            return slice(c * CHUNK, (c + count) * CHUNK)

        def pair_parts(c):
            if c == 0:
                return slice(0, CHUNK // 2), slice(CHUNK // 2, CHUNK)
            return (slice(0, CHUNK),)

        def first_product(c):
            g, place = divmod(c * CHUNK, GATHER)
            banks = {}
            for d in (SECOND, FIRST):
                banks[d] = bank_tile(c % HIDDEN_BANKS + (HIDDEN_BANKS if d == FIRST else 0))
                for t in range(PACK):
                    nc.tensor.matmul_mx(
                        out=banks[d][:, t, :],
                        lhsT=w1_codes[:, t, :].bitcast(FP8X4),
                        lhsT_scale=w1_scales[:, t, :],
                        rhs=picked_words(d * V + c * CHUNK).bitcast(FP8X4),
                        rhs_scale=xs_plane[g][:, d * GATHER + place : d * GATHER + place + CHUNK],
                        start=True,
                        stop=True,
                    )
            second_relu = ring.tile([P, CHUNK, PACK], F32, name="second_relu", bufs=CHUNKS)
            for part in pair_parts(c):
                nc.scalar.activation(
                    out=second_relu[:, part, :],
                    in_=banks[SECOND][:, :, part].rearrange("p t v -> p v t"),
                    func=ACT.Relu,
                )
            return banks[FIRST], second_relu

        def band(c, w, part=slice(0, CHUNK)):
            first_bank, second_relu = hidden[c]
            nc.vector.scalar_tensor_tensor(
                out=band_bf[c][:, w, part, :],
                in0=first_bank[:, :, part].rearrange("p t v -> p v t"),
                scalar=0.0,
                in1=second_relu[:, part, :],
                op0=ALU.max,
                op1=ALU.add if w == LOW else ALU.subtract,
            )

        def quantise_band(c, w):
            nc.vector.quantize_mx(
                out=band_codes[c][w][:].bitcast(FP8X4),
                scales=band_scales[c][w][:],
                in_=band_bf[c][:, w, :, :].rearrange("p v t -> p (v t)"),
            )

        def second_pass(out, c, w, t, start, stop):
            nc.tensor.matmul_mx(
                out=out,
                lhsT=w23[w][:, t, :].bitcast(FP4X4),
                lhsT_scale=w23s[:, w, t, :],
                rhs=band_codes[c][w][:].bitcast(FP8X4),
                rhs_scale=band_scales[c][w][:],
                start=start,
                stop=stop,
            )

        def second_product(c):
            bank = bank_tile(RESULT_BANKS[c])
            for w in (LOW, HIGH):
                for t in range(PACK):
                    second_pass(bank[:, t, :], c, w, t, (w, t) == (LOW, 0), (w, t) == (HIGH, PACK - 1))
            y_f32 = ring.tile([P, PACK, CHUNK], F32, name="y_f32", bufs=CHUNKS)
            nc.scalar.copy(out=y_f32[:], in_=bank[:])
            nc.sync.dma_start(out=y_rows[:, :, columns(c)], in_=y_f32[:])
            return bank, y_f32

        def round_from_bank(c, bank):
            nc.scalar.copy(out=y_bf[:, columns(c), :], in_=bank[:].rearrange("p t v -> p v t"))

        def round_from_sbuf(c, y_f32, part=slice(0, CHUNK)):
            nc.vector.tensor_copy(
                out=y_bf[:, columns(c), :][:, part].rearrange("p (u i) t -> p u t i", i=PACK),
                in_=y_f32[:, :, part].rearrange("p t (u i) -> p u t i", i=PACK),
            )

        def quantise_result(c, part=slice(0, CHUNK)):
            nc.vector.quantize_mx(
                out=y_codes[:, columns(c)][:, part].bitcast(FP8X4),
                scales=y_scales[:, columns(c)][:, part],
                in_=y_bf[:, columns(c), :][:, part].rearrange("p v t -> p (v t)"),
            )

        def store_codes(cols):
            nc.sync.dma_start(out=y_words[:, cols], in_=y_codes[:, cols].bitcast(I32))

        def last_chunk(y_before):
            last = CHUNKS - 1
            banks = [bank_tile(number)[:, 0, :] for number in LAST_RESULT_BANKS]
            quantise_band(last, LOW)
            for t in range(PACK):
                second_pass(banks[t], last, LOW, t, True, False)
            band(last, HIGH)
            quantise_result(0)
            quantise_band(last, HIGH)
            for t in range(PACK):
                second_pass(banks[t], last, HIGH, t, False, True)
            quantise_result(1)
            store_codes(columns(0, 2))
            round_from_sbuf(last - 1, y_before)
            quantise_result(last - 1)
            y_f32 = ring.tile([P, PACK, CHUNK], F32, name="y_f32", bufs=CHUNKS)
            for t in range(PACK):
                if t < PACK // 2:
                    nc.vector.tensor_copy(out=y_f32[:, t, :], in_=banks[t])
                else:
                    nc.scalar.copy(out=y_f32[:, t, :], in_=banks[t])
            nc.scalar.dma_start(out=y_rows[:, :, columns(last)], in_=y_f32[:])
            halves = slice(0, CHUNK // 2), slice(CHUNK // 2, CHUNK)
            for part in halves:
                round_from_sbuf(last, y_f32, part)
            for part in halves:
                quantise_result(last, part)
            store_codes(columns(last - 1, 2))

        y_bf = keep.tile([P, V, PACK], BF16, name="y_bf", align_bytes=64)
        hidden = [first_product(0), first_product(1)]
        for w in (LOW, HIGH):
            deal_words(w, nc.scalar.copy)
        hidden.append(first_product(2))
        band_bf = [
            ring.tile([P, 2, CHUNK, PACK], BF16, name="band_bf", align_bytes=64, bufs=CHUNKS) for c in range(CHUNKS)
        ]
        band_codes = [
            [keep.tile([P, CHUNK], U32, name="band_codes%d_%d" % (c, w), align_bytes=64) for w in (LOW, HIGH)]
            for c in range(CHUNKS)
        ]
        band_scales = [
            [keep.tile([P, CHUNK], U8, name="band_scales%d_%d" % (c, w), align_bytes=64) for w in (LOW, HIGH)]
            for c in range(CHUNKS)
        ]

        for part in pair_parts(0):
            band(0, LOW, part)
        band(0, HIGH)
        hidden.append(first_product(CHUNKS - 1))
        band(1, LOW)
        band(1, HIGH)
        quantise_band(0, LOW)
        quantise_band(0, HIGH)
        round_from_bank(0, second_product(0)[0])
        quantise_band(1, LOW)
        band(2, LOW)
        quantise_band(1, HIGH)
        round_from_bank(1, second_product(1)[0])
        band(2, HIGH)
        quantise_band(2, LOW)
        band(3, LOW)
        quantise_band(2, HIGH)
        last_chunk(second_product(2)[1])

        for quadrant in range(4):
            queue = nc.sync if quadrant < 2 else nc.scalar
            queue.dma_start(
                out=out_2[0, 4 * quadrant : 4 * quadrant + 4, :].bitcast(I32),
                in_=y_scales[32 * quadrant : 32 * quadrant + 4, :].bitcast(I32),
            )
